import numpy as np, ml_dtypes
CORES = [1,5,17,21,33,37,49,53]
N = 8
import mx_ref
BF = ml_dtypes.bfloat16
def gcols(t, e):
    v = np.concatenate([t.reshape(8, 16, -1, 4), np.zeros((8, 16, 1, 4), BF)], axis=2)
    return np.ascontiguousarray(np.stack([v[g][:, e[g]] for g in range(8)])).reshape(128, -1)
def tile(rs):
    return np.stack(rs, axis=2).reshape(128, -1).astype(BF)
def pick(q, e):
    c = np.concatenate([q[0].reshape(128, -1, 4), np.zeros((128, 1, 4), np.uint8)], axis=1); s = np.concatenate([q[1], np.ones((16, 1), np.uint8)], axis=1)
    return (np.ascontiguousarray(c[:, e].reshape(128, -1)), np.ascontiguousarray(s[:, e]))
def join(*qs):
    return (np.concatenate([q[0] for q in qs], axis=1), np.concatenate([q[1] for q in qs], axis=1))
def put(q, e, v):
    c, s = q[0].reshape(128, -1, 4).copy(), q[1].copy(); c[:, e] = v[0].reshape(128, -1, 4); s[:, e] = v[1]
    return (c.reshape(128, -1), s)
def pk(c, s):
    return (np.ascontiguousarray(c), mx_ref.live(s))
def emit(q):
    return q[0], q[1]
def packed(v, rng):
    q = [mx_ref.quantize(np.ascontiguousarray(v[r])) for r in range(N)]
    return np.stack([a for a, b in q]), np.stack([mx_ref.plane(b, rng) for a, b in q])
def values_of_codes():
    e, c = np.zeros((128, 128, 4), np.float32), np.zeros((128, 2, 4), np.uint8)
    e[np.arange(128), np.arange(128), 0] = 1
    c[:127, :, 0] = np.arange(256).reshape(2, 128).T[:127]
    return mx_ref.matmul(mx_ref.quantize(e.reshape(128, 512).astype(BF)), (c.reshape(128, 8), np.full((16, 2), 127, np.uint8))).T.reshape(-1).astype(np.float64)
CODE_VALUE, SCALE_VALUE = values_of_codes(), 2.0 ** (np.arange(256) - 127.0)
def decode(q):
    return (CODE_VALUE[q[0]].reshape(16, 8, -1, 4) * SCALE_VALUE[q[1]][:, None, :, None] + 0.0).reshape(128, -1).astype(np.float32)
def f(rng, *shape):
    return mx_ref.flush((rng.standard_normal(shape, dtype=np.float32) * np.exp2(rng.integers(-2, 3, shape[:-1] + (1,)))).astype(BF))
def wide(rng, *shape, cols=0):
    v = rng.standard_normal(shape, dtype=np.float32) * np.exp2(rng.integers(-12, 13, shape)).astype(np.float32)
    if cols: v *= np.repeat(np.exp2(rng.integers(-cols, cols + 1, shape[:-2] + (1, shape[-1] // 4))) * (rng.random(shape[:-2] + (1, shape[-1] // 4)) > 0.0625), 4, axis=-1).astype(np.float32)
    return mx_ref.flush(v.astype(BF))
C, K, R, TEAM = 320, 128, 3, 4
def big(v):
    v = v.astype(np.float32)
    v[np.abs(v) < np.float32(2.0 ** -16)] = 0
    return v.astype(BF)
def numbers_of(rng):
    return {"x": big(f(rng, N, 128, 4 * C)), "u": np.array(f(rng, N, 128, 512)), "v": np.array(f(rng, N, 128, 512))}
def layers(rng):
    return big(f(rng, N, 128, 2048)).reshape(N, 8, 16, 4, 8, 16, 4)
def weights(rng, w):
    c, p = packed(np.ascontiguousarray(w).reshape(N, 128, 2048), rng)
    return {"wc": c, "ws": p}
def setup_inputs(rng):
    return {**numbers_of(rng), **weights(rng, layers(rng))}
def setup_inputs_ties(rng):
    d = numbers_of(rng)
    e = rng.permutation(N)
    x = d["x"].reshape(N, 8, 16, C, 4)
    k = rng.integers(0, 3, (N, 8, 2, C))
    k[:, :, 1] = np.where(rng.random((N, 8, C)) < 0.5, k[:, :, 0], k[:, :, 1])
    x[:, :, :2] = 0
    x[:, :, :2, :, 0] = k.astype(np.float32).astype(BF)
    u = d["u"].reshape(N, 128, 128, 4)
    u[:, :, ::16] = 0
    u[:, :, 1::16] = 0
    for r in range(N):
        for h in range(0, 128, 16):
            for i in range(2): u[r, h + i, h + i, 0] = 0.0 if r == e[0] else -1.0 if r == e[1] else 1.0
    w = layers(rng)
    w[:, :, :, :, :, :2] = 0
    return {"x": x.reshape(N, 128, 4 * C), "u": u.reshape(N, 128, 512), "v": d["v"], **weights(rng, w)}
def setup_inputs_near(rng):
    d = numbers_of(rng)
    x = d["x"].astype(np.float32).reshape(N, 8, 16, C, 4)
    x[:, :, 0] = 0
    x[:, :, 8:] = 0
    x[:, :, 0, :, 0] = rng.integers(0, 2, (N, 8, C)) * 2.0 - 1.0
    for r in range(N):
        for g in rng.permutation(8)[:4]: x[r, g, 0, rng.integers(C), 0] = 2.0 ** 28 * rng.choice([-1.0, 1.0])
    s = rng.integers(0, 16, (N, 8, 2, C))
    for i in range(2): x[:, :, 8 + 2 * i] = ((s[:, :, i, :, None] >> np.arange(4)) & 1) * np.exp2(np.arange(4) - 26.0)
    x[:, :, 11, :, 0] = 2.0 ** -13
    x[:, :, 12, :, 0] = (rng.integers(0, 2, (N, 8, C)) * 2.0 - 1.0) * 2.0 ** -27
    u = d["u"].reshape(N, 128, 128, 4)
    u[:, :, ::16] = 0
    u[:, :, 1::16] = 0
    o = rng.permutation(N) % 4
    for r in range(N):
        k = (1.0, 2.0 ** -30, 2.0 ** -33, 2.0 ** 20)[o[r]]
        for h in range(0, 128, 16):
            if o[r] != 2:
                u[r, h, h:h + 2, 0] = k
                u[r, h + 11, h:h + 2, 0] = 8 * k
            else:
                u[r, h + 12, h, 0] = 8 * k
                u[r, h + 12, h + 1, 0] = 9 * k
            u[r, h + 8, h] = 8 * k
            u[r, h + 10, h + 1] = 8 * k
    w = layers(rng)
    for i in [0, 8, 9, 10, 11, 12, 13, 14, 15]:
        w[:, :, i] = 0
        w[:, :, :, :, :, i] = 0
    return {"x": x.reshape(N, 128, 4 * C).astype(BF), "u": u.reshape(N, 128, 512), "v": d["v"], **weights(rng, w)}
def setup_inputs_sides(rng):
    d = numbers_of(rng)
    x = d["x"].reshape(N, 8, 16, C, 4)
    h = rng.permutation(8)
    j = int(rng.integers(80, C // 2 - 15))
    a = rng.integers(0, 2, (N, 8, C)) * 2.0 - 1.0
    q = min(128, C // 2 - 30)
    for r in range(N):
        a[r, h[0]] = 1.0
        a[r, h[1]] = -1.0
        a[r, h[2]] = 1.0 if r % 2 == 1 else -1.0
        a[r, h[3]] = -1.0 if r % 2 == 1 else 1.0
        a[r, h[4]] = np.where(np.arange(C) < j, 1.0, -1.0)
        a[r, h[5]] = np.where(np.arange(C) < j, -1.0, 1.0)
        a[r, h[6]] = 1.0 if r % TEAM == 0 else np.where((np.arange(C) + r) % 3 == 0, 1.0, -1.0)
        a[r, h[7], :q] = 1.0
        a[r, h[7], q:q + 16] = np.where((np.arange(16) + r) % TEAM == 0, -1.0, 1.0)
        a[r, h[7], q + 16:2 * q + 24] = -1.0
    x[:, :, 0] = 0
    x[:, :, 0, :, 0] = a.astype(np.float32).astype(BF)
    k = (N, 8, 8, C, 4)
    x[:, :, 8:] = ((2 * rng.integers(0, 8, k) + 1) * np.exp2(-rng.integers(11, 15, k).astype(np.float32)) * (rng.integers(0, 2, k) * 2 - 1)).astype(np.float32).astype(BF)
    x[:, :, 8, :, 0] = 1.96875
    u = d["u"].reshape(N, 128, 128, 4)
    u[:, :, ::16] = 0
    u[:, :, 1::16] = 0
    for i in range(0, 128, 16): u[:, i, i, 0] = 1.0
    w = layers(rng)
    w[:, :, :, :, :, 8:] = 0
    return {"x": x.reshape(N, 128, 4 * C), "u": u.reshape(N, 128, 512), "v": d["v"], **weights(rng, w)}
def setup_inputs_huge(rng):
    d = numbers_of(rng)
    c = rng.integers(0, 2, (N, 1, 1, C, 1)) * 2.0 - 1.0
    x = 1.75 * 2.0 ** 27 * (0.75 + 0.25 * rng.random((N, 8, 16, C, 4))) * c
    a = np.full((8, 16, 8, 2, 4), 2.0 ** 30, np.float32)
    for g in range(8):
        a[(g + 1) % 8, :, g, 0] *= 0.5
        a[g, :, g, 1] *= 0.5
    u = d["u"].reshape(N, 128, 8, 16, 4)
    u[:, :, :, :2] = a.reshape(128, 8, 2, 4).astype(BF)
    w = (layers(rng).astype(np.float32) * np.float32(2.0 ** -8)).astype(BF)
    return {"x": x.astype(np.float32).reshape(N, 128, 4 * C).astype(BF), "u": u.reshape(N, 128, 512), "v": d["v"], **weights(rng, w)}
def setup_inputs_spread(rng):
    d = setup_inputs(rng)
    d["x"] = big(wide(rng, N, 128, 4 * C, cols=6))
    return d
def check_inputs(d):
    b = []
    for k in ("x", "u", "v"):
        a = np.abs(d[k].astype(np.float32))
        if not (np.isfinite(a).all() and ((a == 0) | (a >= 2.0 ** -30) & (a <= 2.0 ** 30)).all()): b.append("a value of " + k)
    none, least, most = [emit(mx_ref.quantize(np.full((128, 16), k, np.float32).astype(BF)))[1][0, 0] for k in (0.0, 2.0 ** -30, 2.0 ** 30)]
    for r in range(N):
        if ((d["wc"][r] == 0x7F) | (d["wc"][r] == 0xFF)).any(): b.append("wc: a code that is no number")
        s = mx_ref.live(d["ws"][r])
        if ((s != none) & ((s < least) | (s > most))).any(): b.append("ws: a scale out of range")
    return b
def reference(x, u, v, wc, ws):
    qu = [mx_ref.quantize(u[r]) for r in range(N)]
    lay = [pk(wc[r], ws[r]) for r in range(N)]
    now = [x[r] for r in range(N)]
    order = np.zeros((N, 8, C), np.int64)
    for t in range(R):
        vote = np.zeros((N, 8, C), np.int64)
        for r in range(N):
            s = mx_ref.matmul(qu[r], mx_ref.quantize(now[r]))
            vote[r] = np.where(s[::16] >= s[1::16], 1, -1)
        for m in range(0, N, TEAM):
            a = vote[m:m + TEAM].transpose(1, 2, 0).reshape(8, C * TEAM)
            standing = np.cumsum(a, axis=1) - a
            leaves = ((standing >= 0) == (a > 0)).reshape(8, C, TEAM).transpose(2, 0, 1)
            order[m:m + TEAM] = np.argsort(np.where(leaves, 2 * C - np.arange(C), np.arange(C)), axis=2, kind="stable")
        came = [decode(mx_ref.quantize(gcols(now[r], order[r][:, C - K:]))).astype(BF) for r in range(N)]
        made = []
        for r in range(N):
            b = np.concatenate([came[r - 1], gcols(now[r], order[r][:, :C - K])], axis=1).astype(np.float32)
            z = (b - np.roll(b, 2 * C, axis=1) * np.float32(0.5)).astype(BF)
            q = mx_ref.quantize(z)
            made.append(tile([mx_ref.matmul(pick(lay[r], np.arange(128 * i, 128 * i + 128)), q) * np.float32(0.03125) + z[:, i::4].astype(np.float32) for i in range(4)]))
        now = made
    y, od = np.zeros((N, 128, C), np.float32), np.zeros((N, 8, C), np.float32)
    oc, osc = np.zeros((N, 128, 4 * C), np.uint8), np.zeros((N, 16, C), np.uint8)
    for r in range(N):
        q = mx_ref.quantize(now[r])
        y[r] = mx_ref.matmul(mx_ref.quantize(v[r]), q)
        od[r] = order[r]
        oc[r], osc[r] = emit(q)
    return {"y": y, "od": od, "oc": oc, "osc": osc}

@@ -1,0 +1,361 @@
+from concourse.bass import DstId, RemoteDMATransfer
+from concourse.mybir import dt, AluOpType, ActivationFunctionType
+
+C, K, R, TEAM = 320, 128, 3, 4
+HC = C // 2
+NB = C // 32
+MSG = 34
+MAGIC = 2064.0
+BANK = 512
+
+SCRATCH = {
+    "xf": ("sbuf", [128, 4 * C], "bfloat16"),
+    "ut": ("sbuf", [128, 512], "bfloat16"), "vt": ("sbuf", [128, 512], "bfloat16"),
+    "qu": ("sbuf", [128, 128], "float8_e4m3fn_x4"), "su": ("sbuf", [128, 128], "uint8"),
+    "qv": ("sbuf", [128, 128], "float8_e4m3fn_x4"), "sv": ("sbuf", [128, 128], "uint8"),
+    "qw": ("sbuf", [128, 512], "float8_e4m3fn_x4"), "sw": ("sbuf", [128, 512], "uint8"),
+    "one128": ("sbuf", [128, 128], "bfloat16"), "ident": ("sbuf", [128, 128], "bfloat16"),
+    "et": ("sbuf", [128, 2048], "bfloat16"),
+    "qe": ("sbuf", [128, 512], "float8_e4m3fn_x4"), "se": ("sbuf", [128, 512], "uint8"),
+    "pi": ("sbuf", [128, 4], "int32"), "cf": ("sbuf", [128, 16], "float32"),
+    "ii": ("sbuf", [128, 32], "float32"), "vi": ("sbuf", [128, 2 * C], "float32"),
+    "val": ("sbuf", [128, 2 * C], "bfloat16"), "cols": ("sbuf", [128, C], "float32"),
+    "mk": ("sbuf", [128, 64], "bfloat16"), "c6": ("sbuf", [128, 64], "bfloat16"),
+    "ones": ("sbuf", [128, 32], "float32"), "neg1": ("sbuf", [128, 32], "bfloat16"),
+    "k320": ("sbuf", [128, 64], "float32"),
+    "st": ("sbuf", [128, C], "float32"),
+    "vp": ("sbuf", [128, 64], "bfloat16"), "vtt": ("sbuf", [128, 96], "bfloat16"),
+    "ab": ("sbuf", [128, 128], "float32"), "gg": ("sbuf", [128, 64], "bfloat16"),
+    "lv": ("sbuf", [128, 64], "bfloat16"), "rr": ("sbuf", [128, 64], "float32"),
+    "t1": ("sbuf", [128, 64], "float32"), "yt": ("sbuf", [128, 128], "float32"),
+    "yp": ("sbuf", [128, 128], "float32"), "cp": ("sbuf", [128, 64], "float32"),
+    "d1": ("sbuf", [128, 64], "float32"), "tm": ("sbuf", [128, 64], "bfloat16"),
+    "ps": ("sbuf", [128, 64], "float32"), "offs": ("sbuf", [128, 40], "uint16"),
+    "lw": ("sbuf", [128, 4 * C], "bfloat16"), "lt": ("sbuf", [128, 896], "bfloat16"),
+    "fo": ("sbuf", [128, 20], "float32"), "go": ("sbuf", [128, 80], "uint16"),
+    "fo2": ("sbuf", [128, 20], "float32"), "go2": ("sbuf", [128, 20], "uint16"),
+    "odr": ("sbuf", [128, C], "float32"),
+    "hh": ("sbuf", [128, 4 * C], "bfloat16"), "zz": ("sbuf", [128, 4 * C], "bfloat16"),
+    "z32": ("sbuf", [128, 4 * C], "bfloat16"), "x32": ("sbuf", [128, 4 * C], "bfloat16"),
+    "qz": ("sbuf", [128, C], "float8_e4m3fn_x4"), "sz": ("sbuf", [128, C], "uint8"),
+    "ys": ("sbuf", [128, C], "float32"),
+    "pp": ("psum", [128, 8 * BANK], "float32"),
+}
+for _r in range(R):
+    SCRATCH["win%d" % _r] = ("sbuf", [128, 8 * C], "bfloat16")
+    SCRATCH["lq%d" % _r] = ("sbuf", [128, C], "float8_e4m3fn_x4")
+    SCRATCH["ls%d" % _r] = ("sbuf", [128, C], "uint8")
+    SCRATCH["cu%d" % _r] = ("sbuf", [128, 64], "float16")
+    SCRATCH["land%d" % _r] = ("sbuf", [128, 8 * MSG], "float16")
+for _r in range(R + 1):
+    SCRATCH["qx%d" % _r] = ("sbuf", [128, C], "float8_e4m3fn_x4")
+    SCRATCH["sx%d" % _r] = ("sbuf", [128, C], "uint8")
+
+SEMAPHORES = (["dve", "act", "pe", "gp", "ldxa", "ldxb", "ldu", "ldw", "ldv", "outs", "outa", "vsent"]
+              + ["varr%d" % r for r in range(R)] + ["barr%d" % r for r in range(R)] + ["bsent%d" % r for r in range(R)])
+
+
+def as_mask(engines):
+    m = 0
+    for e in engines:
+        m |= 1 << e
+    return m
+
+
+def vote_plan(cores, topo, rank):
+    n = len(cores)
+    base = rank - rank % TEAM
+    dsts = [d for d in range(base, base + TEAM) if d != rank] + [(base + TEAM) % n]
+    src = cores[rank]
+    far = [d for d in dsts if topo.chip(cores[d]) != topo.chip(src)]
+    near = [d for d in dsts if d not in far]
+    used = list(topo.engines(src, cores[far[0]]))
+    plan = [(used, far)]
+    if near:
+        plan.append(([e for e in topo.engines(src, cores[near[0]]) if e not in used], near))
+    return plan
+
+
+def rank_program(g, core, T, topo):
+    rank = T.rank_of(core)
+    if rank is None:
+        return
+    cores = list(T.cores)
+    n = len(cores)
+    A = AluOpType
+    COPY, IDENT = ActivationFunctionType.Copy, ActivationFunctionType.Identity
+    S = T.sem
+    V, ACT, PE = g.vector, g.scalar, g.tensor
+    member = rank % TEAM
+    prev, nxt = (rank - 1) % n, (rank + 1) % n
+    plus = member < 2
+    prev_plus = prev % TEAM < 2
+
+    queues = {"dve": V, "act": ACT, "pe": PE, "gp": g, "sync": g.sync}
+    count = {"dve": 0, "act": 0, "pe": 0, "gp": 0}
+    waited = {}
+
+    def wait(q, *tickets):
+        for name, val in tickets:
+            if waited.get((q, name), 0) < val:
+                queues[q].wait_ge(S[name], val)
+                waited[(q, name)] = val
+
+    def done(q, ins):
+        count[q] += 1
+        ins.then_inc(S[q], 1)
+        return (q, count[q])
+
+    def tt(out, a, b, op, *deps):
+        wait("dve", *deps)
+        return done("dve", V.tensor_tensor(out, a, b, op))
+
+    def ts(out, a, s1, op0, *deps):
+        wait("dve", *deps)
+        return done("dve", V.tensor_scalar(out, a, s1, None, op0))
+
+    def ts2(out, a, s1, s2, op0, op1, *deps):
+        wait("dve", *deps)
+        return done("dve", V.tensor_scalar(out, a, s1, s2, op0, op1))
+
+    def scan(out, d0, d1, init, op0, op1, *deps):
+        wait("dve", *deps)
+        return done("dve", V.tensor_tensor_scan(out, d0, d1, init, op0, op1))
+
+    def tr(out, a, *deps):
+        wait("dve", *deps)
+        return done("dve", V.transpose(out, a))
+
+    def cpy(out, a, *deps):
+        wait("dve", *deps)
+        return done("dve", V.tensor_copy(out, a))
+
+    def fill(out, c, *deps):
+        wait("dve", *deps)
+        return done("dve", V.memset(out, c))
+
+    def quant(q, s, a, *deps):
+        wait("dve", *deps)
+        return done("dve", V.quantize_mx(q, s, a))
+
+    def act(out, a, scale, *deps):
+        wait("act", *deps)
+        return done("act", ACT.activation(out, a, COPY, scale=scale))
+
+    def act_bias(out, a, scale, bias, *deps):
+        wait("act", *deps)
+        return done("act", ACT.activation(out, a, IDENT, bias=bias, scale=scale))
+
+    def mm(bank, cols, lq, ls, rq, rs, *deps):
+        wait("pe", *deps)
+        return done("pe", PE.matmul_mx(T.pp[:, bank * BANK:bank * BANK + cols], lq, ls, rq, rs, True, True))
+
+    def half(h):
+        return h * HC, (h + 1) * HC
+
+    g.sync.dma_start(T.win0[:, 4 * C:4 * C + 4 * HC], T.x[:, 0:4 * HC]).then_inc(S.ldxa, 16)
+    g.scalar.dma_start(T.ut[:], T.u[:]).then_inc(S.ldu, 16)
+    g.sync.dma_start(T.win0[:, 4 * C + 4 * HC:8 * C], T.x[:, 4 * HC:4 * C]).then_inc(S.ldxb, 16)
+
+    g_pi = done("gp", g.iota(T.pi[:, 0:1], [[0, 1]], 0, 1))
+    g_vi = done("gp", g.iota(T.vi[:], [[0, 4], [128, NB], [4, 16]], -2 * C, 0, allow_small_or_imprecise_dtypes=True))
+    g_ii = done("gp", g.iota(T.ii[:], [[1, 32]], 0, 0, allow_small_or_imprecise_dtypes=True))
+    k_one = fill(T.one128[:], 1.0)
+    wait("gp", k_one)
+    g_id = done("gp", g.affine_select(T.ident[:], T.one128[:], [[-1, 128]], A.is_equal, 0.0, 0, 1))
+    g_cols = done("gp", g.iota(T.cols[:], [[1, C]], 0, 0, allow_small_or_imprecise_dtypes=True))
+
+    k_mk = fill(T.mk[:], 1.0)
+    fill(T.vp[:], 0.0)
+    fill(T.c6[:, 0:32], 0.0)
+    fill(T.c6[:, 32:64], -0.5)
+    ts(T.pi[:, 1:2], T.pi[:, 0:1], 31, A.bitwise_and, g_pi)
+    k = ts(T.pi[:, 2:3], T.pi[:, 0:1], 16, A.bitwise_and)
+    fill(T.mk[:, NB - 1:NB], 0.0, k_mk)
+    k_h = ts(T.cf[:, 7:8], T.pi[:, 2:3], 4.0, A.mult, k)
+    k = ts2(T.pi[:, 3:4], T.pi[:, 1:2], float(NB), float(-NB), A.is_ge, A.mult)
+    for c in (31, 32 + NB - 1):
+        fill(T.mk[:, c:c + 1], 0.0)
+    k = tt(T.cf[:, 0:1], T.pi[:, 1:2], T.pi[:, 3:4], A.add, k)
+    fill(T.et[:], 0.0)
+    k_const = ts(T.cf[:, 1:2], T.cf[:, 0:1], -16.0, A.mult, k)
+    k_qu = quant(T.qu[:], T.su[:], T.ut[:], ("ldu", 16), k_const)
+    act_bias(T.lw[:, 0:2 * C], T.vi[:], 0.0, float(2 * C), g_vi)
+    act_bias(T.lw[:, 2 * C:4 * C], T.vi[:], 0.0, float(6 * C))
+    a_val = act_bias(T.val[:], T.vi[:], 1.0, T.cf[:, 7:8], k_h)
+    shift = [C + MAGIC - 7.5, MAGIC - 7.5]
+
+    plans = [vote_plan(cores, topo, q) for q in range(n)]
+    arrivals = sum(len(en) for q in range(n) for en, ds in plans[q] if rank in ds)
+    vsent = [0]
+    bulk_mask = topo.mask(core, cores[nxt])
+    bulk_out = 2 * len(topo.engines(core, cores[nxt]))
+    bulk_in = 2 * len(topo.engines(cores[prev], core))
+    rid_n, pid_n = topo.addr(cores[nxt])[0:2]
+
+    k_x = [("ldxa", 16), ("ldxb", 16)]
+    k_qe = None
+    k_qv = None
+    for r in range(R + 1):
+        last = r == R
+        xt, x0 = (T.xf, 0) if last else (T["win%d" % r], 4 * C)
+        qx, sx = T["qx%d" % r], T["sx%d" % r]
+        k_q, p_s = [], []
+        for h in range(2):
+            a, b = half(h)
+            k_q.append(quant(qx[:, a:b], sx[:, a:b], xt[:, x0 + 4 * a:x0 + 4 * b], k_x[h]))
+            if last:
+                p_s.append(mm(4 * h, HC, T.qv[:], T.sv[:], qx[:, a:b], sx[:, a:b], k_q[h], k_qv))
+            else:
+                p_s.append(mm(4 * h, HC, T.qu[:], T.su[:], qx[:, a:b], sx[:, a:b], k_q[h], k_qu))
+        if last:
+            k_y = [cpy(T.ys[:, half(h)[0]:half(h)[1]], T.pp[:, 4 * h * BANK:4 * h * BANK + HC], p_s[h]) for h in range(2)]
+            for h in range(2):
+                a, b = half(h)
+                wait("sync", k_q[h])
+                g.sync.dma_start(T.oc[:, 4 * a:4 * b], qx[:, a:b].bitcast(dt.uint8)).then_inc(S.outs, 16)
+            wait("act", k_q[1])
+            for q in range(4):
+                g.scalar.dma_start(T.osc[4 * q:4 * q + 4, :], sx[32 * q:32 * q + 4, :]).then_inc(S.outa, 16)
+            for h in range(2):
+                a, b = half(h)
+                wait("sync", k_y[h])
+                g.sync.dma_start(T.y[:, a:b], T.ys[:, a:b]).then_inc(S.outs, 16)
+            break
+        win, cu, land = T["win%d" % r], T["cu%d" % r], T["land%d" % r]
+        lq, ls = T["lq%d" % r], T["ls%d" % r]
+        wait("gp", k_q[1])
+        g.remote_dma(ls[:], sx[:], S["barr%d" % r], S["bsent%d" % r], pid_n, rid_n, bulk_mask)
+        k_ta = tr(T.st[:, 0:HC], T.pp[:, 0:HC], p_s[0])
+        k = tr(T.st[:, HC:C], T.pp[:, 4 * BANK:4 * BANK + HC], p_s[1])
+        for e in range(2):
+            k2 = tt(T.vp[:, 32 + NB * e:32 + NB * e + NB], T.st[:, 16 * e:C:32], T.st[:, 16 * e + 1:C:32],
+                    A.is_ge if plus else A.is_lt, k)
+        k = scan(T.vp[:, 1:2 * NB], T.vp[:, 32:32 + 2 * NB - 1], T.mk[:, 0:2 * NB - 1], 0.0, A.add, A.mult, k2)
+        k = tr(T.vtt[:, 0:64], T.vp[:], k)
+        k_cu = scan(cu[:], T.vtt[:, 0:64], T.c6[:], T.cf[:, 1:2], A.add, A.add, k)
+        wait("gp", k_cu)
+        transfers = []
+        for en, ds in plans[rank]:
+            transfers.append(RemoteDMATransfer(
+                dst_ids=[DstId(rid=topo.addr(cores[d])[0], pnc=topo.addr(cores[d])[1]) for d in ds],
+                dma_engine_mask=as_mask(en), remote_sem=S["varr%d" % r], srcs=[cu[:, 64 - MSG:64]],
+                dsts=[land[:, MSG * rank:MSG * rank + MSG] for d in ds]))
+            vsent[0] += len(en)
+        g.remote_dma_fused(transfers, local_sem=S.vsent)
+        g.remote_dma(lq[:].bitcast(dt.uint8), qx[:].bitcast(dt.uint8), S["barr%d" % r], S["bsent%d" % r],
+                     pid_n, rid_n, bulk_mask)
+        if r == 0:
+            for b in range(4):
+                k = cpy(T.et[:, 512 * b + b:512 * b + 512:4], T.ident[:], g_id)
+            fill(T.ones[:], 1.0)
+            fill(T.neg1[:], -1.0)
+            fill(T.cp[:, 0:1], 0.0)
+            for l in range(2):
+                ts2(T.cf[:, 2 + l:3 + l], T.cf[:, 0:1], -32.0, 1.0 - shift[l], A.mult, A.add)
+                ts2(T.cf[:, 4 + l:5 + l], T.cf[:, 0:1], 32.0, 31.0 + shift[l], A.mult, A.add)
+            k = ts2(T.cf[:, 6:7], T.cf[:, 0:1], -32.0, float(C), A.mult, A.add)
+            k_qe = quant(T.qe[:], T.se[:], T.et[:], k)
+            for l in range(2):
+                k = ts2(T.k320[:, 32 * l:32 * l + 32], T.ii[:], -1.0, T.cf[:, 6:7], A.mult, A.add, g_ii)
+            wait("dve", k, a_val)
+            wait("sync", ("bsent0", bulk_out))
+            g.sync.dma_start(T.qw[:].bitcast(dt.uint8), T.wc[:]).then_inc(S.ldw, 16)
+            g.sync.dma_start(T.sw[:], T.ws[:]).then_inc(S.ldw, 16)
+            g.sync.dma_start(T.vt[:], T.v[:]).then_inc(S.ldv, 16)
+        else:
+            fill(T.lw[:, 384:2 * C], float(2 * C))
+            fill(T.lw[:, 2 * C:(4 * C if r == R - 1 else 1024)], float(6 * C))
+            if r == 1:
+                k_qv = quant(T.qv[:], T.sv[:], T.vt[:], ("ldv", 16))
+        a_d = None
+        for b in range(4):
+            p = mm(b, C, T.qe[:, 128 * b:128 * b + 128], T.se[:, 128 * b:128 * b + 128], lq[:], ls[:],
+                   ("barr%d" % r, bulk_in), k_qe, k_ta)
+            a_d = act(win[:, b:4 * C:4], T.pp[:, b * BANK:b * BANK + C], 1.0, p)
+
+        def term(q, inclusive):
+            o = 2 if inclusive else 1
+            if q == rank:
+                return cu[:, 64 - MSG + o:64 - MSG + o + 32]
+            return land[:, MSG * q + o:MSG * q + o + 32]
+
+        wait("dve", ("varr%d" % r, arrivals), k_cu)
+        for l, who in enumerate((rank, prev)):
+            tb, m = who - who % TEAM, who % TEAM
+            for s in range(2):
+                k = tt(T.ab[:, 64 * s + 32 * l:64 * s + 32 * l + 32], term(tb + 2 * s, 2 * s < m),
+                       term(tb + 2 * s + 1, 2 * s + 1 < m), A.add)
+        k2 = tt(T.vtt[:, 64:96], term(prev, True), term(prev, False), A.is_gt if plus == prev_plus else A.is_lt)
+        k = tt(T.gg[:], T.ab[:, 0:64], T.ab[:, 64:128], A.is_ge, k)
+        k = tt(T.lv[:], T.gg[:], T.vtt[:, 32:96], A.is_equal if plus else A.not_equal, k)
+        for l in range(2):
+            k2 = scan(T.rr[:, 32 * l:32 * l + 32], T.lv[:, 32 * l:32 * l + 32], T.neg1[:], T.cf[:, 2 + l:3 + l],
+                      A.add, A.add, k)
+        k = tt(T.t1[:], T.lv[:], T.k320[:], A.mult)
+        for l in range(2):
+            ts2(T.yt[:, 64 + 32 * l:96 + 32 * l], T.ones[:], T.rr[:, 32 * l + 31:32 * l + 32], T.cf[:, 4 + l:5 + l],
+                A.mult, A.add, k2)
+        k = tt(T.yt[:, 0:64], T.t1[:], T.rr[:], A.subtract, k)
+        k = tr(T.yp[:], T.yt[:], k)
+        wide = 32 + 2 * NB
+        k = scan(T.cp[:, 1:wide], T.yp[:, 64:64 + wide - 1], T.mk[:, 0:wide - 1], 0.0, A.add, A.mult, k)
+        tt(T.d1[:, 0:wide], T.yp[:, 0:wide], T.cp[:, 0:wide], A.subtract, k)
+        k = tt(T.tm[:, 0:wide], T.yp[:, 0:wide], T.cp[:, 0:wide], A.subtract)
+        k = tt(T.ps[:, 0:wide], T.d1[:, 0:wide], T.tm[:, 0:wide], A.add, k)
+        for l in range(2):
+            for e in range(2):
+                k2 = ts(T.offs[:, 2 * NB * l + NB * e:2 * NB * l + NB * e + NB],
+                        T.ps[:, 32 * l + NB * e:32 * l + NB * e + NB], 16.0 * e - 2 * MAGIC + 7.5, A.add, k)
+        k = cpy(T.lw[:].indirect(T.offs[:]), T.val[:], k2)
+        k = tr(T.lt[:, 0:2 * C], T.lw[:, 384:1024], k)
+        k = tt(T.fo[:], T.lt[:, 0:2 * C:32], T.lt[:, 16:2 * C:32], A.add, k)
+        k_go = [ts(T.go[:, 20 * t:20 * t + 20], T.fo[:], float(t), A.add, k) for t in range(4)]
+        k_od = None
+        if r == R - 1:
+            k = tr(T.lt[:, 2 * C:896], T.lw[:, 1024:4 * C])
+            k = tt(T.fo2[:], T.lt[:, 256:896:32], T.lt[:, 272:896:32], A.add, k)
+            k_od = ts2(T.go2[:], T.fo2[:], float(4 * C), 0.25, A.subtract, A.mult, k)
+        a_h = []
+        for h in range(2):
+            o = 1 - h
+            for t in range(4):
+                a_h.append(act(T.hh[:, C * t + HC * o:C * t + HC * o + HC],
+                               win[:].indirect(T.go[:, 20 * t + NB * o:20 * t + NB * o + NB]), 0.5, k_go[t], a_d))
+        k_z, k_qz, p_r = [], [], []
+        for h in range(2):
+            a, b = half(h)
+            o = 1 - h
+            for t in range(4):
+                k = tt(T.zz[:, 4 * a + t:4 * b:4], win[:].indirect(T.go[:, 20 * t + NB * h:20 * t + NB * h + NB]),
+                       T.hh[:, C * t + HC * o:C * t + HC * o + HC], A.subtract, a_h[4 * h + t], k_go[3])
+            k_z.append(k)
+            k_qz.append(quant(T.qz[:, a:b], T.sz[:, a:b], T.zz[:, 4 * a:4 * b], k))
+            for bb in range(4):
+                p_r.append(mm(4 * h + bb, HC, T.qw[:, 128 * bb:128 * bb + 128], T.sw[:, 128 * bb:128 * bb + 128],
+                              T.qz[:, a:b], T.sz[:, a:b], k_qz[h], ("ldw", 32)))
+        xn, n0 = (T.xf, 0) if r == R - 1 else (T["win%d" % (r + 1)], 4 * C)
+        a_z = [act(T.z32[:, 4 * half(h)[0]:4 * half(h)[1]], T.zz[:, 4 * half(h)[0]:4 * half(h)[1]], 32.0, k_z[h])
+               for h in range(2)]
+        k_add = []
+        for h in range(2):
+            a, b = half(h)
+            for bb in range(4):
+                k = tt(T.x32[:, 4 * a + bb:4 * b:4], T.pp[:, (4 * h + bb) * BANK:(4 * h + bb) * BANK + HC],
+                       T.z32[:, 4 * a + bb:4 * b:4], A.add, p_r[4 * h + bb], a_z[h])
+            k_add.append(k)
+        a_x = act(xn[:, n0:n0 + 4 * HC], T.x32[:, 0:4 * HC], 1.0 / 32, k_add[0])
+        k_xb = ts(xn[:, n0 + 4 * HC:n0 + 4 * C], T.x32[:, 4 * HC:4 * C], 1.0 / 32, A.mult, k_add[1])
+        k_x = [a_x, k_xb]
+        if r == R - 1:
+            a_od = act(T.odr[:], T.cols[:].indirect(T.go2[:]), 1.0, k_od, g_cols)
+            wait("act", a_od)
+            g.scalar.dma_start(T.od[:], T.odr[0:128:16, :]).then_inc(S.outa, 16)
+
+    g.sync.wait_ge(S.outs, 64)
+    g.scalar.wait_ge(S.outa, 80)
+    g.wait_ge(S.vsent, vsent[0])
+    for r in range(R):
+        g.wait_ge(S["bsent%d" % r], bulk_out)
+    for q in ("dve", "act", "pe", "gp"):
+        wait("gp", (q, count[q]))

@@ -4,12 +4,15 @@ from concourse.mybir import dt, AluOpType, ActivationFunctionType
 C, K, R, TEAM = 320, 128, 3, 4
 HC = C // 2
 NB = C // 32
+HOME = C - K
+BOTH = HC - K
+LH, LT = HOME // 16, K // 16
 MSG = 34
 MAGIC = 2064.0
 BANK = 512
 
 SCRATCH = {
-    "xf": ("sbuf", [128, 4 * C], "bfloat16"),
+    "x0": ("sbuf", [128, 4 * C], "bfloat16"), "xt": ("sbuf", [128, 4 * C], "bfloat16"),
     "ut": ("sbuf", [128, 512], "bfloat16"), "vt": ("sbuf", [128, 512], "bfloat16"),
     "qu": ("sbuf", [128, 128], "float8_e4m3fn_x4"), "su": ("sbuf", [128, 128], "uint8"),
     "qv": ("sbuf", [128, 128], "float8_e4m3fn_x4"), "sv": ("sbuf", [128, 128], "uint8"),
@@ -18,41 +21,41 @@ SCRATCH = {
     "et": ("sbuf", [128, 2048], "bfloat16"),
     "qe": ("sbuf", [128, 512], "float8_e4m3fn_x4"), "se": ("sbuf", [128, 512], "uint8"),
     "pi": ("sbuf", [128, 4], "int32"), "cf": ("sbuf", [128, 16], "float32"),
-    "ii": ("sbuf", [128, 32], "float32"), "vi": ("sbuf", [128, 2 * C], "float32"),
-    "val": ("sbuf", [128, 2 * C], "bfloat16"), "cols": ("sbuf", [128, C], "float32"),
-    "mk": ("sbuf", [128, 64], "bfloat16"), "c6": ("sbuf", [128, 64], "bfloat16"),
-    "ones": ("sbuf", [128, 32], "float32"), "neg1": ("sbuf", [128, 32], "bfloat16"),
-    "k320": ("sbuf", [128, 64], "float32"),
+    "ii": ("sbuf", [128, 32], "float32"), "vi": ("sbuf", [128, C], "float32"),
+    "val": ("sbuf", [128, C], "bfloat16"), "cols": ("sbuf", [128, C], "float32"),
+    "mk": ("sbuf", [128, 32], "bfloat16"), "c6": ("sbuf", [128, 64], "bfloat16"),
+    "cst": ("sbuf", [128, 64], "float32"), "k320": ("sbuf", [128, 32], "float32"),
     "st": ("sbuf", [128, C], "float32"),
-    "vp": ("sbuf", [128, 64], "bfloat16"), "vtt": ("sbuf", [128, 96], "bfloat16"),
-    "ab": ("sbuf", [128, 128], "float32"), "gg": ("sbuf", [128, 64], "bfloat16"),
-    "lv": ("sbuf", [128, 64], "bfloat16"), "rr": ("sbuf", [128, 64], "float32"),
-    "t1": ("sbuf", [128, 64], "float32"), "yt": ("sbuf", [128, 128], "float32"),
-    "yp": ("sbuf", [128, 128], "float32"), "cp": ("sbuf", [128, 64], "float32"),
-    "d1": ("sbuf", [128, 64], "float32"), "tm": ("sbuf", [128, 64], "bfloat16"),
-    "ps": ("sbuf", [128, 64], "float32"), "offs": ("sbuf", [128, 40], "uint16"),
-    "lw": ("sbuf", [128, 4 * C], "bfloat16"), "lt": ("sbuf", [128, 896], "bfloat16"),
-    "fo": ("sbuf", [128, 20], "float32"), "go": ("sbuf", [128, 80], "uint16"),
-    "fo2": ("sbuf", [128, 20], "float32"), "go2": ("sbuf", [128, 20], "uint16"),
+    "vp": ("sbuf", [128, 64], "bfloat16"), "vtt": ("sbuf", [128, 64], "bfloat16"),
+    "ab": ("sbuf", [128, 64], "float32"), "gg": ("sbuf", [128, 32], "bfloat16"),
+    "lv": ("sbuf", [128, 64], "bfloat16"), "yt": ("sbuf", [128, 96], "float32"),
+    "yp": ("sbuf", [128, 96], "float32"), "cp": ("sbuf", [128, 32], "float32"), "yl": ("sbuf", [128, 32], "float32"),
+    "d1": ("sbuf", [128, 32], "float32"), "tm": ("sbuf", [128, 32], "bfloat16"),
+    "ps": ("sbuf", [128, 32], "float32"), "offs": ("sbuf", [128, 2 * NB], "uint16"),
+    "lw": ("sbuf", [128, 2 * C], "bfloat16"), "lt": ("sbuf", [128, 2 * C], "bfloat16"),
+    "fo": ("sbuf", [128, 2 * NB], "float32"),
     "odr": ("sbuf", [128, C], "float32"),
-    "hh": ("sbuf", [128, 4 * C], "bfloat16"), "zz": ("sbuf", [128, 4 * C], "bfloat16"),
+    "dd": ("sbuf", [128, 4 * C], "bfloat16"), "hd": ("sbuf", [128, 4 * K], "bfloat16"),
+    "hh": ("sbuf", [128, 4 * HOME], "bfloat16"), "gh": ("sbuf", [128, 4 * HOME], "bfloat16"),
+    "zz": ("sbuf", [128, 4 * C], "bfloat16"),
     "z32": ("sbuf", [128, 4 * C], "bfloat16"), "x32": ("sbuf", [128, 4 * C], "bfloat16"),
     "qz": ("sbuf", [128, C], "float8_e4m3fn_x4"), "sz": ("sbuf", [128, C], "uint8"),
     "ys": ("sbuf", [128, C], "float32"),
     "pp": ("psum", [128, 8 * BANK], "float32"),
 }
 for _r in range(R):
-    SCRATCH["win%d" % _r] = ("sbuf", [128, 8 * C], "bfloat16")
     SCRATCH["lq%d" % _r] = ("sbuf", [128, C], "float8_e4m3fn_x4")
     SCRATCH["ls%d" % _r] = ("sbuf", [128, C], "uint8")
     SCRATCH["cu%d" % _r] = ("sbuf", [128, 64], "float16")
-    SCRATCH["land%d" % _r] = ("sbuf", [128, 8 * MSG], "float16")
+    SCRATCH["land%d" % _r] = ("sbuf", [128, TEAM * MSG], "float16")
+    SCRATCH["go%d" % _r] = ("sbuf", [128, LH + LT], "uint16")
+    SCRATCH["came%d" % _r] = ("sbuf", [128, LT], "uint16")
 for _r in range(R + 1):
     SCRATCH["qx%d" % _r] = ("sbuf", [128, C], "float8_e4m3fn_x4")
     SCRATCH["sx%d" % _r] = ("sbuf", [128, C], "uint8")
 
-SEMAPHORES = (["dve", "act", "pe", "gp", "ldxa", "ldxb", "ldu", "ldw", "ldv", "outs", "outa", "vsent"]
-              + ["varr%d" % r for r in range(R)] + ["barr%d" % r for r in range(R)] + ["bsent%d" % r for r in range(R)])
+SEMAPHORES = (["dve", "act", "pe", "gp", "ldxa", "ldxb", "ldu", "ldw", "ldv", "outs", "outa", "sent"]
+              + [s % r for r in range(R) for s in ("varr%d", "barr%d", "larr%d")])
 
 
 def as_mask(engines):
@@ -63,16 +66,16 @@ def as_mask(engines):
 
 
 def vote_plan(cores, topo, rank):
-    n = len(cores)
     base = rank - rank % TEAM
-    dsts = [d for d in range(base, base + TEAM) if d != rank] + [(base + TEAM) % n]
+    dsts = [d for d in range(base, base + TEAM) if d != rank]
     src = cores[rank]
     far = [d for d in dsts if topo.chip(cores[d]) != topo.chip(src)]
     near = [d for d in dsts if d not in far]
     used = list(topo.engines(src, cores[far[0]]))
     plan = [(used, far)]
     if near:
-        plan.append(([e for e in topo.engines(src, cores[near[0]]) if e not in used], near))
+        free = [e for e in topo.engines(src, cores[near[0]]) if e not in used]
+        plan.append((free[:len(used) * len(near) // len(far)], near))
     return plan
 
 
@@ -89,7 +92,6 @@ def rank_program(g, core, T, topo):
     member = rank % TEAM
     prev, nxt = (rank - 1) % n, (rank + 1) % n
     plus = member < 2
-    prev_plus = prev % TEAM < 2
 
     queues = {"dve": V, "act": ACT, "pe": PE, "gp": g, "sync": g.sync}
     count = {"dve": 0, "act": 0, "pe": 0, "gp": 0}
@@ -153,17 +155,22 @@ def rank_program(g, core, T, topo):
     def half(h):
         return h * HC, (h + 1) * HC
 
-    g.sync.dma_start(T.win0[:, 4 * C:4 * C + 4 * HC], T.x[:, 0:4 * HC]).then_inc(S.ldxa, 16)
+    def plane(buf, t, a=0, b=C):
+        return buf[:, C * t + a:C * t + b]
+
+    g.sync.dma_start(T.x0[:, 0:4 * HC], T.x[:, 0:4 * HC]).then_inc(S.ldxa, 16)
     g.scalar.dma_start(T.ut[:], T.u[:]).then_inc(S.ldu, 16)
-    g.sync.dma_start(T.win0[:, 4 * C + 4 * HC:8 * C], T.x[:, 4 * HC:4 * C]).then_inc(S.ldxb, 16)
+    g.sync.dma_start(T.x0[:, 4 * HC:4 * C], T.x[:, 4 * HC:4 * C]).then_inc(S.ldxb, 16)
+    wait("sync", ("ldxa", 16))
+    g.sync.dma_start(T.qw[:].bitcast(dt.uint8), T.wc[:]).then_inc(S.ldw, 16)
+    g.sync.dma_start(T.sw[:], T.ws[:]).then_inc(S.ldw, 16)
 
     g_pi = done("gp", g.iota(T.pi[:, 0:1], [[0, 1]], 0, 1))
-    g_vi = done("gp", g.iota(T.vi[:], [[0, 4], [128, NB], [4, 16]], -2 * C, 0, allow_small_or_imprecise_dtypes=True))
     g_ii = done("gp", g.iota(T.ii[:], [[1, 32]], 0, 0, allow_small_or_imprecise_dtypes=True))
     k_one = fill(T.one128[:], 1.0)
     wait("gp", k_one)
     g_id = done("gp", g.affine_select(T.ident[:], T.one128[:], [[-1, 128]], A.is_equal, 0.0, 0, 1))
-    g_cols = done("gp", g.iota(T.cols[:], [[1, C]], 0, 0, allow_small_or_imprecise_dtypes=True))
+    g_vi = done("gp", g.iota(T.vi[:], [[0, 2], [32, NB], [1, 16]], -HC, 0, allow_small_or_imprecise_dtypes=True))
 
     k_mk = fill(T.mk[:], 1.0)
     fill(T.vp[:], 0.0)
@@ -172,42 +179,53 @@ def rank_program(g, core, T, topo):
     ts(T.pi[:, 1:2], T.pi[:, 0:1], 31, A.bitwise_and, g_pi)
     k = ts(T.pi[:, 2:3], T.pi[:, 0:1], 16, A.bitwise_and)
     fill(T.mk[:, NB - 1:NB], 0.0, k_mk)
-    k_h = ts(T.cf[:, 7:8], T.pi[:, 2:3], 4.0, A.mult, k)
+    k_h = cpy(T.cf[:, 7:8], T.pi[:, 2:3], k)
     k = ts2(T.pi[:, 3:4], T.pi[:, 1:2], float(NB), float(-NB), A.is_ge, A.mult)
-    for c in (31, 32 + NB - 1):
-        fill(T.mk[:, c:c + 1], 0.0)
+    k_et = fill(T.et[:], 0.0)
     k = tt(T.cf[:, 0:1], T.pi[:, 1:2], T.pi[:, 3:4], A.add, k)
-    fill(T.et[:], 0.0)
+    cpy(T.et[:, 0:512:4], T.ident[:], g_id, k_et)
     k_const = ts(T.cf[:, 1:2], T.cf[:, 0:1], -16.0, A.mult, k)
+    for b in range(1, 4):
+        cpy(T.et[:, 512 * b + b:512 * b + 512:4], T.ident[:])
     k_qu = quant(T.qu[:], T.su[:], T.ut[:], ("ldu", 16), k_const)
-    act_bias(T.lw[:, 0:2 * C], T.vi[:], 0.0, float(2 * C), g_vi)
-    act_bias(T.lw[:, 2 * C:4 * C], T.vi[:], 0.0, float(6 * C))
-    a_val = act_bias(T.val[:], T.vi[:], 1.0, T.cf[:, 7:8], k_h)
-    shift = [C + MAGIC - 7.5, MAGIC - 7.5]
+    a_val = act_bias(T.val[:], T.vi[:], 1.0, T.cf[:, 7:8], g_vi, k_h)
+    for t in range(4):
+        a_x32 = act(plane(T.x32, t), T.x0[:, t:4 * C:4], 32.0, ("ldxa", 16), ("ldxb", 16))
+    shift = MAGIC - 7.5
 
     plans = [vote_plan(cores, topo, q) for q in range(n)]
     arrivals = sum(len(en) for q in range(n) for en, ds in plans[q] if rank in ds)
-    vsent = [0]
-    bulk_mask = topo.mask(core, cores[nxt])
-    bulk_out = 2 * len(topo.engines(core, cores[nxt]))
-    bulk_in = 2 * len(topo.engines(cores[prev], core))
+    sent = [0]
     rid_n, pid_n = topo.addr(cores[nxt])[0:2]
 
-    k_x = [("ldxa", 16), ("ldxb", 16)]
+    def bulk(src, dst):
+        return plans[src][0][0], list(topo.engines(cores[src], cores[dst]))
+
+    def to_next(dst, src, sem, engines):
+        g.remote_dma(dst, src, sem, S.sent, pid_n, rid_n, as_mask(engines))
+        sent[0] += len(engines)
+
+    en_plane, en_codes = bulk(rank, nxt)
+    in_plane, in_codes = [len(e) for e in bulk(prev, rank)]
+
+    k_x = [[("ldxa", 16)], [("ldxb", 16)]]
+    late = []
     k_qe = None
     k_qv = None
     for r in range(R + 1):
         last = r == R
-        xt, x0 = (T.xf, 0) if last else (T["win%d" % r], 4 * C)
+        xt = T.x0 if r == 0 else T.xt
         qx, sx = T["qx%d" % r], T["sx%d" % r]
         k_q, p_s = [], []
         for h in range(2):
             a, b = half(h)
-            k_q.append(quant(qx[:, a:b], sx[:, a:b], xt[:, x0 + 4 * a:x0 + 4 * b], k_x[h]))
+            k_q.append(quant(qx[:, a:b], sx[:, a:b], xt[:, 4 * a:4 * b], *k_x[h]))
             if last:
                 p_s.append(mm(4 * h, HC, T.qv[:], T.sv[:], qx[:, a:b], sx[:, a:b], k_q[h], k_qv))
             else:
                 p_s.append(mm(4 * h, HC, T.qu[:], T.su[:], qx[:, a:b], sx[:, a:b], k_q[h], k_qu))
+            if h == 0:
+                k_x[1] = k_x[1] + [call() for call in late]
         if last:
             k_y = [cpy(T.ys[:, half(h)[0]:half(h)[1]], T.pp[:, 4 * h * BANK:4 * h * BANK + HC], p_s[h]) for h in range(2)]
             for h in range(2):
@@ -222,140 +240,131 @@ def rank_program(g, core, T, topo):
                 wait("sync", k_y[h])
                 g.sync.dma_start(T.y[:, a:b], T.ys[:, a:b]).then_inc(S.outs, 16)
             break
-        win, cu, land = T["win%d" % r], T["cu%d" % r], T["land%d" % r]
+        cu, land, go, came = T["cu%d" % r], T["land%d" % r], T["go%d" % r], T["came%d" % r]
         lq, ls = T["lq%d" % r], T["ls%d" % r]
         wait("gp", k_q[1])
-        g.remote_dma(ls[:], sx[:], S["barr%d" % r], S["bsent%d" % r], pid_n, rid_n, bulk_mask)
+        to_next(ls[:], sx[:], S["barr%d" % r], en_plane)
         k_ta = tr(T.st[:, 0:HC], T.pp[:, 0:HC], p_s[0])
         k = tr(T.st[:, HC:C], T.pp[:, 4 * BANK:4 * BANK + HC], p_s[1])
         for e in range(2):
             k2 = tt(T.vp[:, 32 + NB * e:32 + NB * e + NB], T.st[:, 16 * e:C:32], T.st[:, 16 * e + 1:C:32],
                     A.is_ge if plus else A.is_lt, k)
         k = scan(T.vp[:, 1:2 * NB], T.vp[:, 32:32 + 2 * NB - 1], T.mk[:, 0:2 * NB - 1], 0.0, A.add, A.mult, k2)
-        k = tr(T.vtt[:, 0:64], T.vp[:], k)
-        k_cu = scan(cu[:], T.vtt[:, 0:64], T.c6[:], T.cf[:, 1:2], A.add, A.add, k)
+        k = tr(T.vtt[:], T.vp[:], k)
+        k_cu = scan(cu[:], T.vtt[:], T.c6[:], T.cf[:, 1:2], A.add, A.add, k)
         wait("gp", k_cu)
         transfers = []
         for en, ds in plans[rank]:
             transfers.append(RemoteDMATransfer(
                 dst_ids=[DstId(rid=topo.addr(cores[d])[0], pnc=topo.addr(cores[d])[1]) for d in ds],
                 dma_engine_mask=as_mask(en), remote_sem=S["varr%d" % r], srcs=[cu[:, 64 - MSG:64]],
-                dsts=[land[:, MSG * rank:MSG * rank + MSG] for d in ds]))
-            vsent[0] += len(en)
-        g.remote_dma_fused(transfers, local_sem=S.vsent)
-        g.remote_dma(lq[:].bitcast(dt.uint8), qx[:].bitcast(dt.uint8), S["barr%d" % r], S["bsent%d" % r],
-                     pid_n, rid_n, bulk_mask)
+                dsts=[land[:, MSG * member:MSG * member + MSG] for d in ds]))
+            sent[0] += len(en)
+        g.remote_dma_fused(transfers, local_sem=S.sent)
+        to_next(lq[:].bitcast(dt.uint8), qx[:].bitcast(dt.uint8), S["barr%d" % r], en_codes)
+        fill(T.lw[:], float(HC))
         if r == 0:
-            for b in range(4):
-                k = cpy(T.et[:, 512 * b + b:512 * b + 512:4], T.ident[:], g_id)
-            fill(T.ones[:], 1.0)
-            fill(T.neg1[:], -1.0)
+            fill(T.cst[:, 0:32], -1.0)
+            fill(T.cst[:, 33:64], 0.0)
+            fill(T.lv[:, 32:64], 0.0)
             fill(T.cp[:, 0:1], 0.0)
-            for l in range(2):
-                ts2(T.cf[:, 2 + l:3 + l], T.cf[:, 0:1], -32.0, 1.0 - shift[l], A.mult, A.add)
-                ts2(T.cf[:, 4 + l:5 + l], T.cf[:, 0:1], 32.0, 31.0 + shift[l], A.mult, A.add)
+            ts2(T.cf[:, 2:3], T.cf[:, 0:1], -32.0, 1.0 - shift, A.mult, A.add)
+            ts2(T.cst[:, 32:33], T.cf[:, 0:1], 32.0, 31.0 + shift, A.mult, A.add)
             k = ts2(T.cf[:, 6:7], T.cf[:, 0:1], -32.0, float(C), A.mult, A.add)
-            k_qe = quant(T.qe[:], T.se[:], T.et[:], k)
-            for l in range(2):
-                k = ts2(T.k320[:, 32 * l:32 * l + 32], T.ii[:], -1.0, T.cf[:, 6:7], A.mult, A.add, g_ii)
-            wait("dve", k, a_val)
-            wait("sync", ("bsent0", bulk_out))
-            g.sync.dma_start(T.qw[:].bitcast(dt.uint8), T.wc[:]).then_inc(S.ldw, 16)
-            g.sync.dma_start(T.sw[:], T.ws[:]).then_inc(S.ldw, 16)
-            g.sync.dma_start(T.vt[:], T.v[:]).then_inc(S.ldv, 16)
-        else:
-            fill(T.lw[:, 384:2 * C], float(2 * C))
-            fill(T.lw[:, 2 * C:(4 * C if r == R - 1 else 1024)], float(6 * C))
-            if r == 1:
-                k_qv = quant(T.qv[:], T.sv[:], T.vt[:], ("ldv", 16))
+            k_qe = quant(T.qe[:], T.se[:], T.et[:])
+            k = ts2(T.k320[:], T.ii[:], -1.0, T.cf[:, 6:7], A.mult, A.add, g_ii, k)
+            wait("dve", k, a_val, a_x32)
+        if r == 1:
+            k_qv = quant(T.qv[:], T.sv[:], T.vt[:], ("ldv", 16))
+        if r == R - 1:
+            g_cols = done("gp", g.iota(T.cols[:], [[1, C]], 0, 0, allow_small_or_imprecise_dtypes=True))
         a_d = None
         for b in range(4):
             p = mm(b, C, T.qe[:, 128 * b:128 * b + 128], T.se[:, 128 * b:128 * b + 128], lq[:], ls[:],
-                   ("barr%d" % r, bulk_in), k_qe, k_ta)
-            a_d = act(win[:, b:4 * C:4], T.pp[:, b * BANK:b * BANK + C], 1.0, p)
+                   ("barr%d" % r, in_plane + in_codes), k_qe, k_ta)
+            a_d = act(plane(T.dd, b), T.pp[:, b * BANK:b * BANK + C], 1.0, p)
 
-        def term(q, inclusive):
-            o = 2 if inclusive else 1
-            if q == rank:
+        def term(m):
+            o = 2 if m < member else 1
+            if m == member:
                 return cu[:, 64 - MSG + o:64 - MSG + o + 32]
-            return land[:, MSG * q + o:MSG * q + o + 32]
+            return land[:, MSG * m + o:MSG * m + o + 32]
 
         wait("dve", ("varr%d" % r, arrivals), k_cu)
-        for l, who in enumerate((rank, prev)):
-            tb, m = who - who % TEAM, who % TEAM
-            for s in range(2):
-                k = tt(T.ab[:, 64 * s + 32 * l:64 * s + 32 * l + 32], term(tb + 2 * s, 2 * s < m),
-                       term(tb + 2 * s + 1, 2 * s + 1 < m), A.add)
-        k2 = tt(T.vtt[:, 64:96], term(prev, True), term(prev, False), A.is_gt if plus == prev_plus else A.is_lt)
-        k = tt(T.gg[:], T.ab[:, 0:64], T.ab[:, 64:128], A.is_ge, k)
-        k = tt(T.lv[:], T.gg[:], T.vtt[:, 32:96], A.is_equal if plus else A.not_equal, k)
-        for l in range(2):
-            k2 = scan(T.rr[:, 32 * l:32 * l + 32], T.lv[:, 32 * l:32 * l + 32], T.neg1[:], T.cf[:, 2 + l:3 + l],
-                      A.add, A.add, k)
-        k = tt(T.t1[:], T.lv[:], T.k320[:], A.mult)
-        for l in range(2):
-            ts2(T.yt[:, 64 + 32 * l:96 + 32 * l], T.ones[:], T.rr[:, 32 * l + 31:32 * l + 32], T.cf[:, 4 + l:5 + l],
-                A.mult, A.add, k2)
-        k = tt(T.yt[:, 0:64], T.t1[:], T.rr[:], A.subtract, k)
+        for s in range(2):
+            k = tt(T.ab[:, 32 * s:32 * s + 32], term(2 * s), term(2 * s + 1), A.add)
+        k = tt(T.gg[:], T.ab[:, 0:32], T.ab[:, 32:64], A.is_ge, k)
+        k = tt(T.lv[:, 0:32], T.gg[:], T.vtt[:, 32:64], A.is_equal if plus else A.not_equal, k)
+        scan(T.yt[:, 32:96], T.lv[:], T.cst[:], T.cf[:, 2:3], A.add, A.add, k)
+        k = tt(T.yt[:, 0:32], T.lv[:, 0:32], T.k320[:], A.mult)
         k = tr(T.yp[:], T.yt[:], k)
-        wide = 32 + 2 * NB
-        k = scan(T.cp[:, 1:wide], T.yp[:, 64:64 + wide - 1], T.mk[:, 0:wide - 1], 0.0, A.add, A.mult, k)
-        tt(T.d1[:, 0:wide], T.yp[:, 0:wide], T.cp[:, 0:wide], A.subtract, k)
-        k = tt(T.tm[:, 0:wide], T.yp[:, 0:wide], T.cp[:, 0:wide], A.subtract)
+        wide = 2 * NB
+        scan(T.cp[:, 1:wide], T.yp[:, 64:64 + wide - 1], T.mk[:, 0:wide - 1], 0.0, A.add, A.mult, k)
+        k = tt(T.yl[:, 0:wide], T.yp[:, 0:wide], T.yp[:, 32:32 + wide], A.subtract)
+        tt(T.d1[:, 0:wide], T.yl[:, 0:wide], T.cp[:, 0:wide], A.subtract, k)
+        k = tt(T.tm[:, 0:wide], T.yl[:, 0:wide], T.cp[:, 0:wide], A.subtract)
         k = tt(T.ps[:, 0:wide], T.d1[:, 0:wide], T.tm[:, 0:wide], A.add, k)
-        for l in range(2):
-            for e in range(2):
-                k2 = ts(T.offs[:, 2 * NB * l + NB * e:2 * NB * l + NB * e + NB],
-                        T.ps[:, 32 * l + NB * e:32 * l + NB * e + NB], 16.0 * e - 2 * MAGIC + 7.5, A.add, k)
+        for e in range(2):
+            k2 = ts(T.offs[:, NB * e:NB * e + NB], T.ps[:, NB * e:NB * e + NB], 16.0 * e - 2 * MAGIC + 7.5, A.add, k)
         k = cpy(T.lw[:].indirect(T.offs[:]), T.val[:], k2)
-        k = tr(T.lt[:, 0:2 * C], T.lw[:, 384:1024], k)
-        k = tt(T.fo[:], T.lt[:, 0:2 * C:32], T.lt[:, 16:2 * C:32], A.add, k)
-        k_go = [ts(T.go[:, 20 * t:20 * t + 20], T.fo[:], float(t), A.add, k) for t in range(4)]
-        k_od = None
-        if r == R - 1:
-            k = tr(T.lt[:, 2 * C:896], T.lw[:, 1024:4 * C])
-            k = tt(T.fo2[:], T.lt[:, 256:896:32], T.lt[:, 272:896:32], A.add, k)
-            k_od = ts2(T.go2[:], T.fo2[:], float(4 * C), 0.25, A.subtract, A.mult, k)
-        a_h = []
-        for h in range(2):
-            o = 1 - h
-            for t in range(4):
-                a_h.append(act(T.hh[:, C * t + HC * o:C * t + HC * o + HC],
-                               win[:].indirect(T.go[:, 20 * t + NB * o:20 * t + NB * o + NB]), 0.5, k_go[t], a_d))
-        k_z, k_qz, p_r = [], [], []
+        k = tr(T.lt[:, 32 * LH:2 * C], T.lw[:, 32 * LH:2 * C], k)
+        k2 = tr(T.lt[:, 0:32 * LH], T.lw[:, 0:32 * LH])
+        k = tt(T.fo[:, LH:LH + LT], T.lt[:, 32 * LH:2 * C:32], T.lt[:, 32 * LH + 16:2 * C:32], A.add, k)
+        k2 = tt(T.fo[:, 0:LH], T.lt[:, 0:32 * LH:32], T.lt[:, 16:32 * LH:32], A.add, k2)
+        k_gt = cpy(go[:, LH:LH + LT], T.fo[:, LH:LH + LT], k)
+        k_gh = cpy(go[:, 0:LH], T.fo[:, 0:LH], k2)
+        wait("gp", k_gt)
+        to_next(came[:], go[:, LH:LH + LT], S["larr%d" % r], en_codes)
+        for t in range(2):
+            k = ts(T.hh[:, t:4 * HOME:4], plane(T.x32, t).indirect(go[:, 0:LH]), 1.0 / 64, A.mult, k_gh)
+            a_h = act(T.hh[:, t + 2:4 * HOME:4], plane(T.x32, t + 2).indirect(go[:, 0:LH]), 1.0 / 64, k_gh)
+        a_g = act(T.gh[:, 4 * BOTH:4 * HC], T.hh[:, 4 * BOTH:4 * HC], 2.0, k, a_h)
+        ts(T.gh[:, 0:4 * BOTH], T.hh[:, 0:4 * BOTH], 2.0, A.mult, k, a_h)
+        k = ts(T.gh[:, 4 * HC:4 * HOME], T.hh[:, 4 * HC:4 * HOME], 2.0, A.mult)
+        tt(T.zz[:, 4 * K:4 * HC], T.gh[:, 0:4 * BOTH], T.hh[:, 4 * HC:4 * HOME], A.subtract, k)
+        tt(T.zz[:, 4 * (HC + K):4 * C], T.gh[:, 4 * HC:4 * HOME], T.hh[:, 0:4 * BOTH], A.subtract)
+        listed = ("larr%d" % r, in_codes)
+        if r == 0:
+            wait("sync", listed)
+            g.sync.dma_start(T.vt[:], T.v[:]).then_inc(S.ldv, 16)
+        for t in range(4):
+            a_hd = act(T.hd[:, t:4 * K:4], plane(T.dd, t).indirect(came[:]), 0.5, listed, a_d)
+        k_z, p_r = [], []
         for h in range(2):
             a, b = half(h)
-            o = 1 - h
-            for t in range(4):
-                k = tt(T.zz[:, 4 * a + t:4 * b:4], win[:].indirect(T.go[:, 20 * t + NB * h:20 * t + NB * h + NB]),
-                       T.hh[:, C * t + HC * o:C * t + HC * o + HC], A.subtract, a_h[4 * h + t], k_go[3])
+            if h == 0:
+                for t in range(4):
+                    k = tt(T.zz[:, t:4 * K:4], plane(T.dd, t).indirect(came[:]), T.hh[:, 4 * BOTH + t:4 * HC:4],
+                           A.subtract, listed, a_d)
+            else:
+                k = tt(T.zz[:, 4 * HC:4 * (HC + K)], T.gh[:, 4 * BOTH:4 * HC], T.hd[:], A.subtract, a_g, a_hd)
             k_z.append(k)
-            k_qz.append(quant(T.qz[:, a:b], T.sz[:, a:b], T.zz[:, 4 * a:4 * b], k))
+            k = quant(T.qz[:, a:b], T.sz[:, a:b], T.zz[:, 4 * a:4 * b], k)
             for bb in range(4):
                 p_r.append(mm(4 * h + bb, HC, T.qw[:, 128 * bb:128 * bb + 128], T.sw[:, 128 * bb:128 * bb + 128],
-                              T.qz[:, a:b], T.sz[:, a:b], k_qz[h], ("ldw", 32)))
-        xn, n0 = (T.xf, 0) if r == R - 1 else (T["win%d" % (r + 1)], 4 * C)
-        a_z = [act(T.z32[:, 4 * half(h)[0]:4 * half(h)[1]], T.zz[:, 4 * half(h)[0]:4 * half(h)[1]], 32.0, k_z[h])
-               for h in range(2)]
+                              T.qz[:, a:b], T.sz[:, a:b], k, ("ldw", 32)))
+        a_z = []
+        for h in range(2):
+            a, b = half(h)
+            a_z.append(act(T.z32[:, 4 * a:4 * b], T.zz[:, 4 * a:4 * b], 32.0, k_z[h]))
+            if h == 0 and r == R - 1:
+                a_od = act(T.odr[:], T.cols[:].indirect(go[:]), 1.0, k_gt, g_cols)
+                wait("sync", a_od)
+                g.sync.dma_start(T.od[:], T.odr[0:128:16, :]).then_inc(S.outs, 16)
         k_add = []
         for h in range(2):
             a, b = half(h)
             for bb in range(4):
-                k = tt(T.x32[:, 4 * a + bb:4 * b:4], T.pp[:, (4 * h + bb) * BANK:(4 * h + bb) * BANK + HC],
-                       T.z32[:, 4 * a + bb:4 * b:4], A.add, p_r[4 * h + bb], a_z[h])
-            k_add.append(k)
-        a_x = act(xn[:, n0:n0 + 4 * HC], T.x32[:, 0:4 * HC], 1.0 / 32, k_add[0])
-        k_xb = ts(xn[:, n0 + 4 * HC:n0 + 4 * C], T.x32[:, 4 * HC:4 * C], 1.0 / 32, A.mult, k_add[1])
-        k_x = [a_x, k_xb]
-        if r == R - 1:
-            a_od = act(T.odr[:], T.cols[:].indirect(T.go2[:]), 1.0, k_od, g_cols)
-            wait("act", a_od)
-            g.scalar.dma_start(T.od[:], T.odr[0:128:16, :]).then_inc(S.outa, 16)
+                k_add.append(tt(plane(T.x32, bb, a, b), T.pp[:, (4 * h + bb) * BANK:(4 * h + bb) * BANK + HC],
+                                T.z32[:, 4 * a + bb:4 * b:4], A.add, p_r[4 * h + bb], a_z[h]))
+        a_x = [act(T.xt[:, 4 * half(i // 4)[0] + i % 4:4 * half(i // 4)[1]:4], plane(T.x32, i % 4, *half(i // 4)),
+                   1.0 / 32, k_add[i]) for i in range(6)]
+        k_x = [[a_x[3]], [a_x[5]]]
+        late = [lambda bb=bb, k=k_add[4 + bb]: ts(T.xt[:, 4 * HC + bb:4 * C:4], plane(T.x32, bb, HC, C), 1.0 / 32,
+                                                  A.mult, k) for bb in (2, 3)]
 
-    g.sync.wait_ge(S.outs, 64)
-    g.scalar.wait_ge(S.outa, 80)
-    g.wait_ge(S.vsent, vsent[0])
-    for r in range(R):
-        g.wait_ge(S["bsent%d" % r], bulk_out)
+    g.sync.wait_ge(S.outs, 80)
+    g.scalar.wait_ge(S.outa, 64)
+    g.wait_ge(S.sent, sent[0])
     for q in ("dve", "act", "pe", "gp"):
         wait("gp", (q, count[q]))

@@ -8,8 +8,13 @@ HOME = C - K
 BOTH = HC - K
 LH, LT = HOME // 16, K // 16
 MSG = 34
-MAGIC = 2064.0
+UNIT = 4096.0
+WHOLE = 1.5 * 2 ** 23 * UNIT
+ROUND = 16 * WHOLE
+FIVE = 5 * 32
+STEPS = 7
 BANK = 512
+EARLY, NACT, WLATE = True, 5, False
 
 SCRATCH = {
     "x0": ("sbuf", [128, 4 * C], "bfloat16"), "xt": ("sbuf", [128, 4 * C], "bfloat16"),
@@ -24,14 +29,14 @@ SCRATCH = {
     "ii": ("sbuf", [128, 32], "float32"), "vi": ("sbuf", [128, C], "float32"),
     "val": ("sbuf", [128, C], "bfloat16"), "cols": ("sbuf", [128, C], "float32"),
     "mk": ("sbuf", [128, 32], "bfloat16"), "c6": ("sbuf", [128, 64], "bfloat16"),
-    "cst": ("sbuf", [128, 64], "float32"), "k320": ("sbuf", [128, 32], "float32"),
-    "st": ("sbuf", [128, C], "float32"),
+    "zr": ("sbuf", [128, FIVE + 32], "bfloat16"), "st": ("sbuf", [128, C], "float32"),
     "vp": ("sbuf", [128, 64], "bfloat16"), "vtt": ("sbuf", [128, 64], "bfloat16"),
-    "ab": ("sbuf", [128, 64], "float32"), "gg": ("sbuf", [128, 32], "bfloat16"),
-    "lv": ("sbuf", [128, 64], "bfloat16"), "yt": ("sbuf", [128, 96], "float32"),
-    "yp": ("sbuf", [128, 96], "float32"), "cp": ("sbuf", [128, 32], "float32"), "yl": ("sbuf", [128, 32], "float32"),
-    "d1": ("sbuf", [128, 32], "float32"), "tm": ("sbuf", [128, 32], "bfloat16"),
-    "ps": ("sbuf", [128, 32], "float32"), "offs": ("sbuf", [128, 2 * NB], "uint16"),
+    "own": ("sbuf", [128, 64], "float32"), "mq": ("sbuf", [128, FIVE + 32], "float32"),
+    "pa": ("sbuf", [128, FIVE + 32], "bfloat16"), "pb": ("sbuf", [128, FIVE], "float32"),
+    "oa": ("sbuf", [128, FIVE + 32], "float32"), "ob": ("sbuf", [128, FIVE], "float32"),
+    "yp": ("sbuf", [128, 96], "float32"), "mkn": ("sbuf", [128, 32], "bfloat16"),
+    "sq": ("sbuf", [128, STEPS * 2 * NB], "float32"), "so": ("sbuf", [128, STEPS * 2 * NB], "float32"),
+    "pat": ("sbuf", [128, STEPS * 2 * NB], "float32"), "offs": ("sbuf", [128, 2 * NB], "uint16"),
     "lw": ("sbuf", [128, 2 * C], "bfloat16"), "lt": ("sbuf", [128, 2 * C], "bfloat16"),
     "fo": ("sbuf", [128, 2 * NB], "float32"),
     "odr": ("sbuf", [128, C], "float32"),
@@ -91,7 +96,6 @@ def rank_program(g, core, T, topo):
     V, ACT, PE = g.vector, g.scalar, g.tensor
     member = rank % TEAM
     prev, nxt = (rank - 1) % n, (rank + 1) % n
-    plus = member < 2
 
     queues = {"dve": V, "act": ACT, "pe": PE, "gp": g, "sync": g.sync}
     count = {"dve": 0, "act": 0, "pe": 0, "gp": 0}
@@ -161,9 +165,14 @@ def rank_program(g, core, T, topo):
     g.sync.dma_start(T.x0[:, 0:4 * HC], T.x[:, 0:4 * HC]).then_inc(S.ldxa, 16)
     g.scalar.dma_start(T.ut[:], T.u[:]).then_inc(S.ldu, 16)
     g.sync.dma_start(T.x0[:, 4 * HC:4 * C], T.x[:, 4 * HC:4 * C]).then_inc(S.ldxb, 16)
-    wait("sync", ("ldxa", 16))
-    g.sync.dma_start(T.qw[:].bitcast(dt.uint8), T.wc[:]).then_inc(S.ldw, 16)
-    g.sync.dma_start(T.sw[:], T.ws[:]).then_inc(S.ldw, 16)
+
+    def load_layer(ticket):
+        wait("sync", ticket)
+        g.sync.dma_start(T.qw[:].bitcast(dt.uint8), T.wc[:]).then_inc(S.ldw, 16)
+        g.sync.dma_start(T.sw[:], T.ws[:]).then_inc(S.ldw, 16)
+
+    if not WLATE:
+        load_layer(("ldxa", 16))
 
     g_pi = done("gp", g.iota(T.pi[:, 0:1], [[0, 1]], 0, 1))
     g_ii = done("gp", g.iota(T.ii[:], [[1, 32]], 0, 0, allow_small_or_imprecise_dtypes=True))
@@ -172,6 +181,7 @@ def rank_program(g, core, T, topo):
     g_id = done("gp", g.affine_select(T.ident[:], T.one128[:], [[-1, 128]], A.is_equal, 0.0, 0, 1))
     g_vi = done("gp", g.iota(T.vi[:], [[0, 2], [32, NB], [1, 16]], -HC, 0, allow_small_or_imprecise_dtypes=True))
 
+    k_zr = fill(T.zr[:], 0.0)
     k_mk = fill(T.mk[:], 1.0)
     fill(T.vp[:], 0.0)
     fill(T.c6[:, 0:32], 0.0)
@@ -181,17 +191,37 @@ def rank_program(g, core, T, topo):
     fill(T.mk[:, NB - 1:NB], 0.0, k_mk)
     k_h = cpy(T.cf[:, 7:8], T.pi[:, 2:3], k)
     k = ts2(T.pi[:, 3:4], T.pi[:, 1:2], float(NB), float(-NB), A.is_ge, A.mult)
-    k_et = fill(T.et[:], 0.0)
+    fill(T.et[:, 0:1024], 0.0)
     k = tt(T.cf[:, 0:1], T.pi[:, 1:2], T.pi[:, 3:4], A.add, k)
-    cpy(T.et[:, 0:512:4], T.ident[:], g_id, k_et)
+    fill(T.et[:, 1024:2048], 0.0)
     k_const = ts(T.cf[:, 1:2], T.cf[:, 0:1], -16.0, A.mult, k)
-    for b in range(1, 4):
-        cpy(T.et[:, 512 * b + b:512 * b + 512:4], T.ident[:])
-    k_qu = quant(T.qu[:], T.su[:], T.ut[:], ("ldu", 16), k_const)
+    k_qu = quant(T.qu[:], T.su[:], T.ut[:], ("ldu", 16))
+
+    def const(buf, a, b, step, c, *deps):
+        return act_bias(buf[:, a:b:step], T.zr[:, 0:len(range(a, b, step))], 1.0, c, k_zr, *deps)
+
+    wide = 2 * NB
+    a = const(T.pat, 0, STEPS * wide, 1, 1.0)
+    a = const(T.pb, 0, FIVE, 1, 1.0)
+    const(T.pa, 0, FIVE + 32, 1, 1.0)
+    for o, c in ((2, WHOLE), (3, -WHOLE), (4, -UNIT)):
+        const(T.mq, o, FIVE, 5, c)
+    const(T.mq, FIVE + 1, FIVE + 32, 1, 0.0)
+    const(T.pat, 0, STEPS * wide, STEPS, 0.0, a)
+    const(T.pb, 0, FIVE, 5, 0.0)
+    const(T.sq, 1, STEPS, 5, 0.0)
+    const(T.sq, 2, STEPS * wide, STEPS, -7.5 * UNIT)
+    const(T.sq, 3, STEPS * wide, STEPS, ROUND)
+    for e in range(2):
+        const(T.sq, STEPS * NB * e + 4, STEPS * NB * (e + 1), STEPS, 16 * e * UNIT - ROUND)
+    a = act_bias(T.cf[:, 6:7], T.cf[:, 0:1], -32.0, float(C), k_const)
+    act(T.cf[:, 2:3], T.cf[:, 0:1], -32.0 * UNIT)
+    act_bias(T.mq[:, FIVE:FIVE + 1], T.cf[:, 0:1], 32.0 * UNIT, 32.0 * UNIT)
+    act(T.mkn[:], T.mk[:], -1.0)
+    act_bias(T.pb[:, 4:FIVE:5], T.ii[:], -1.0, T.cf[:, 6:7], g_ii, a)
     a_val = act_bias(T.val[:], T.vi[:], 1.0, T.cf[:, 7:8], g_vi, k_h)
     for t in range(4):
-        a_x32 = act(plane(T.x32, t), T.x0[:, t:4 * C:4], 32.0, ("ldxa", 16), ("ldxb", 16))
-    shift = MAGIC - 7.5
+        a_xp = act(plane(T.x32, t), T.x0[:, t:4 * C:4], 32.0, ("ldxa", 16), ("ldxb", 16))
 
     plans = [vote_plan(cores, topo, q) for q in range(n)]
     arrivals = sum(len(en) for q in range(n) for en, ds in plans[q] if rank in ds)
@@ -205,11 +235,10 @@ def rank_program(g, core, T, topo):
         g.remote_dma(dst, src, sem, S.sent, pid_n, rid_n, as_mask(engines))
         sent[0] += len(engines)
 
-    en_plane, en_codes = bulk(rank, nxt)
-    in_plane, in_codes = [len(e) for e in bulk(prev, rank)]
+    en_early, en_codes = bulk(rank, nxt)
+    in_early, in_codes = [len(e) for e in bulk(prev, rank)]
 
     k_x = [[("ldxa", 16)], [("ldxb", 16)]]
-    late = []
     k_qe = None
     k_qv = None
     for r in range(R + 1):
@@ -224,8 +253,9 @@ def rank_program(g, core, T, topo):
                 p_s.append(mm(4 * h, HC, T.qv[:], T.sv[:], qx[:, a:b], sx[:, a:b], k_q[h], k_qv))
             else:
                 p_s.append(mm(4 * h, HC, T.qu[:], T.su[:], qx[:, a:b], sx[:, a:b], k_q[h], k_qu))
-            if h == 0:
-                k_x[1] = k_x[1] + [call() for call in late]
+            if not last and h == (0 if r == 0 and EARLY else 1):
+                wait("gp", k_q[h])
+                to_next(T["ls%d" % r][:, 0:b], sx[:, 0:b], S["barr%d" % r], en_early)
         if last:
             k_y = [cpy(T.ys[:, half(h)[0]:half(h)[1]], T.pp[:, 4 * h * BANK:4 * h * BANK + HC], p_s[h]) for h in range(2)]
             for h in range(2):
@@ -242,16 +272,14 @@ def rank_program(g, core, T, topo):
             break
         cu, land, go, came = T["cu%d" % r], T["land%d" % r], T["go%d" % r], T["came%d" % r]
         lq, ls = T["lq%d" % r], T["ls%d" % r]
-        wait("gp", k_q[1])
-        to_next(ls[:], sx[:], S["barr%d" % r], en_plane)
         k_ta = tr(T.st[:, 0:HC], T.pp[:, 0:HC], p_s[0])
         k = tr(T.st[:, HC:C], T.pp[:, 4 * BANK:4 * BANK + HC], p_s[1])
         for e in range(2):
             k2 = tt(T.vp[:, 32 + NB * e:32 + NB * e + NB], T.st[:, 16 * e:C:32], T.st[:, 16 * e + 1:C:32],
-                    A.is_ge if plus else A.is_lt, k)
+                    A.is_ge, k)
         k = scan(T.vp[:, 1:2 * NB], T.vp[:, 32:32 + 2 * NB - 1], T.mk[:, 0:2 * NB - 1], 0.0, A.add, A.mult, k2)
         k = tr(T.vtt[:], T.vp[:], k)
-        k_cu = scan(cu[:], T.vtt[:], T.c6[:], T.cf[:, 1:2], A.add, A.add, k)
+        k_cu = scan(cu[:], T.vtt[:], T.c6[:], T.cf[:, 1:2], A.add, A.add, k, k_const)
         wait("gp", k_cu)
         transfers = []
         for en, ds in plans[rank]:
@@ -262,18 +290,20 @@ def rank_program(g, core, T, topo):
             sent[0] += len(en)
         g.remote_dma_fused(transfers, local_sem=S.sent)
         to_next(lq[:].bitcast(dt.uint8), qx[:].bitcast(dt.uint8), S["barr%d" % r], en_codes)
+        if r == 0 and EARLY:
+            to_next(ls[:, HC:C], sx[:, HC:C], S["barr%d" % r], en_codes)
+        k = ts2(T.own[:, 32:64], T.vtt[:, 32:64], UNIT, 0.25 - UNIT / 2, A.mult, A.add)
+        for sign in (T.pa[:, 0:FIVE:5], T.pa[:, 2:FIVE:5], T.pb[:, 2:FIVE:5]):
+            ts2(sign, T.vtt[:, 32:64], 2.0, -1.0, A.mult, A.add, a_val)
+        k_own = tt(T.own[:, 0:32], T.own[:, 32:64], cu[:, 64 - MSG + 1:64 - MSG + 33], A.add, k, k_cu)
         fill(T.lw[:], float(HC))
         if r == 0:
-            fill(T.cst[:, 0:32], -1.0)
-            fill(T.cst[:, 33:64], 0.0)
-            fill(T.lv[:, 32:64], 0.0)
-            fill(T.cp[:, 0:1], 0.0)
-            ts2(T.cf[:, 2:3], T.cf[:, 0:1], -32.0, 1.0 - shift, A.mult, A.add)
-            ts2(T.cst[:, 32:33], T.cf[:, 0:1], 32.0, 31.0 + shift, A.mult, A.add)
-            k = ts2(T.cf[:, 6:7], T.cf[:, 0:1], -32.0, float(C), A.mult, A.add)
-            k_qe = quant(T.qe[:], T.se[:], T.et[:])
-            k = ts2(T.k320[:], T.ii[:], -1.0, T.cf[:, 6:7], A.mult, A.add, g_ii, k)
-            wait("dve", k, a_val, a_x32)
+            for b in range(4):
+                k_et = cpy(T.et[:, 512 * b + b:512 * b + 512:4], T.ident[:], g_id)
+            k_qe = quant(T.qe[:], T.se[:], T.et[:], k_et)
+            wait("dve", a_xp)
+            if WLATE:
+                load_layer(("varr0", arrivals))
         if r == 1:
             k_qv = quant(T.qv[:], T.sv[:], T.vt[:], ("ldv", 16))
         if r == R - 1:
@@ -281,32 +311,29 @@ def rank_program(g, core, T, topo):
         a_d = None
         for b in range(4):
             p = mm(b, C, T.qe[:, 128 * b:128 * b + 128], T.se[:, 128 * b:128 * b + 128], lq[:], ls[:],
-                   ("barr%d" % r, in_plane + in_codes), k_qe, k_ta)
+                   ("barr%d" % r, in_early + (2 if r == 0 and EARLY else 1) * in_codes), k_qe, k_ta)
             a_d = act(plane(T.dd, b), T.pp[:, b * BANK:b * BANK + C], 1.0, p)
 
         def term(m):
             o = 2 if m < member else 1
-            if m == member:
-                return cu[:, 64 - MSG + o:64 - MSG + o + 32]
             return land[:, MSG * m + o:MSG * m + o + 32]
 
-        wait("dve", ("varr%d" % r, arrivals), k_cu)
-        for s in range(2):
-            k = tt(T.ab[:, 32 * s:32 * s + 32], term(2 * s), term(2 * s + 1), A.add)
-        k = tt(T.gg[:], T.ab[:, 0:32], T.ab[:, 32:64], A.is_ge, k)
-        k = tt(T.lv[:, 0:32], T.gg[:], T.vtt[:, 32:64], A.is_equal if plus else A.not_equal, k)
-        scan(T.yt[:, 32:96], T.lv[:], T.cst[:], T.cf[:, 2:3], A.add, A.add, k)
-        k = tt(T.yt[:, 0:32], T.lv[:, 0:32], T.k320[:], A.mult)
-        k = tr(T.yp[:], T.yt[:], k)
-        wide = 2 * NB
-        scan(T.cp[:, 1:wide], T.yp[:, 64:64 + wide - 1], T.mk[:, 0:wide - 1], 0.0, A.add, A.mult, k)
-        k = tt(T.yl[:, 0:wide], T.yp[:, 0:wide], T.yp[:, 32:32 + wide], A.subtract)
-        tt(T.d1[:, 0:wide], T.yl[:, 0:wide], T.cp[:, 0:wide], A.subtract, k)
-        k = tt(T.tm[:, 0:wide], T.yl[:, 0:wide], T.cp[:, 0:wide], A.subtract)
-        k = tt(T.ps[:, 0:wide], T.d1[:, 0:wide], T.tm[:, 0:wide], A.add, k)
-        for e in range(2):
-            k2 = ts(T.offs[:, NB * e:NB * e + NB], T.ps[:, NB * e:NB * e + NB], 16.0 * e - 2 * MAGIC + 7.5, A.add, k)
-        k = cpy(T.lw[:].indirect(T.offs[:]), T.val[:], k2)
+        mates = [m for m in range(TEAM) if m != member]
+        tt(T.mq[:, 0:FIVE:5], T.own[:, 0:32], term(mates[0]), A.add, ("varr%d" % r, arrivals), k_own)
+        k = tt(T.mq[:, 1:FIVE:5], term(mates[1]), term(mates[2]), A.add)
+        k = scan(T.oa[:], T.pa[:], T.mq[:], T.cf[:, 2:3], A.mult, A.add, k)
+        k2 = scan(T.ob[:], T.pb[:], T.mq[:, 0:FIVE], 0.0, A.mult, A.add)
+        k = tr(T.yp[:, 64:96], T.oa[:, FIVE:FIVE + 32], k)
+        tr(T.yp[:, 32:64], T.oa[:, 4:FIVE:5])
+        k2 = tr(T.yp[:, 0:32], T.ob[:, 4:FIVE:5], k2)
+        for o in (1, 6):
+            scan(T.sq[:, STEPS + o:STEPS * wide:STEPS], T.yp[:, 64:64 + wide - 1], T.mkn[:, 0:wide - 1], 0.0,
+                 A.subtract, A.mult, k)
+        for o in (0, 5):
+            k = tt(T.sq[:, o:STEPS * wide:STEPS], T.yp[:, 0:wide], T.yp[:, 32:32 + wide], A.subtract, k2)
+        k = scan(T.so[:], T.pat[:], T.sq[:], 0.0, A.mult, A.add, k)
+        k = ts(T.offs[:], T.so[:, STEPS - 1:STEPS * wide:STEPS], 1.0 / UNIT, A.mult, k)
+        k = cpy(T.lw[:].indirect(T.offs[:]), T.val[:], k)
         k = tr(T.lt[:, 32 * LH:2 * C], T.lw[:, 32 * LH:2 * C], k)
         k2 = tr(T.lt[:, 0:32 * LH], T.lw[:, 0:32 * LH])
         k = tt(T.fo[:, LH:LH + LT], T.lt[:, 32 * LH:2 * C:32], T.lt[:, 32 * LH + 16:2 * C:32], A.add, k)
@@ -315,53 +342,66 @@ def rank_program(g, core, T, topo):
         k_gh = cpy(go[:, 0:LH], T.fo[:, 0:LH], k2)
         wait("gp", k_gt)
         to_next(came[:], go[:, LH:LH + LT], S["larr%d" % r], en_codes)
-        for t in range(2):
-            k = ts(T.hh[:, t:4 * HOME:4], plane(T.x32, t).indirect(go[:, 0:LH]), 1.0 / 64, A.mult, k_gh)
-            a_h = act(T.hh[:, t + 2:4 * HOME:4], plane(T.x32, t + 2).indirect(go[:, 0:LH]), 1.0 / 64, k_gh)
-        a_g = act(T.gh[:, 4 * BOTH:4 * HC], T.hh[:, 4 * BOTH:4 * HC], 2.0, k, a_h)
-        ts(T.gh[:, 0:4 * BOTH], T.hh[:, 0:4 * BOTH], 2.0, A.mult, k, a_h)
-        k = ts(T.gh[:, 4 * HC:4 * HOME], T.hh[:, 4 * HC:4 * HOME], 2.0, A.mult)
-        tt(T.zz[:, 4 * K:4 * HC], T.gh[:, 0:4 * BOTH], T.hh[:, 4 * HC:4 * HOME], A.subtract, k)
-        tt(T.zz[:, 4 * (HC + K):4 * C], T.gh[:, 4 * HC:4 * HOME], T.hh[:, 0:4 * BOTH], A.subtract)
+        k_h = [ts(T.hh[:, t:4 * HOME:4], plane(T.x32, t).indirect(go[:, 0:LH]), 1.0 / 64, A.mult, k_gh) for t in (0, 1)]
+        k_h += [act(T.hh[:, t:4 * HOME:4], plane(T.x32, t).indirect(go[:, 0:LH]), 1.0 / 64, k_gh) for t in (2, 3)]
+        if r == R - 1:
+            a_od = act(T.odr[:], T.cols[:].indirect(go[:]), 1.0, g_cols)
+            wait("sync", a_od)
+            g.sync.dma_start(T.od[:], T.odr[0:128:16, :]).then_inc(S.outs, 16)
+        for t in (0, 2, 1, 3):
+            k_g = ts(T.gh[:, t:4 * HOME:4], T.hh[:, t:4 * HOME:4], 2.0, A.mult, k_h[t])
         listed = ("larr%d" % r, in_codes)
         if r == 0:
             wait("sync", listed)
             g.sync.dma_start(T.vt[:], T.v[:]).then_inc(S.ldv, 16)
-        for t in range(4):
-            a_hd = act(T.hd[:, t:4 * K:4], plane(T.dd, t).indirect(came[:]), 0.5, listed, a_d)
-        k_z, p_r = [], []
-        for h in range(2):
-            a, b = half(h)
-            if h == 0:
-                for t in range(4):
-                    k = tt(T.zz[:, t:4 * K:4], plane(T.dd, t).indirect(came[:]), T.hh[:, 4 * BOTH + t:4 * HC:4],
+        a_hd = [act(T.hd[:, t:4 * K:4], plane(T.dd, t).indirect(came[:]), 0.5, listed, a_d) for t in range(4)]
+        k_z, a_z, p_r, k_add = {}, {}, {}, []
+
+        def z_came(t):
+            k_z[0, t] = tt(T.zz[:, t:4 * K:4], plane(T.dd, t).indirect(came[:]), T.hh[:, 4 * BOTH + t:4 * HC:4],
                            A.subtract, listed, a_d)
-            else:
-                k = tt(T.zz[:, 4 * HC:4 * (HC + K)], T.gh[:, 4 * BOTH:4 * HC], T.hd[:], A.subtract, a_g, a_hd)
-            k_z.append(k)
-            k = quant(T.qz[:, a:b], T.sz[:, a:b], T.zz[:, 4 * a:4 * b], k)
-            for bb in range(4):
-                p_r.append(mm(4 * h + bb, HC, T.qw[:, 128 * bb:128 * bb + 128], T.sw[:, 128 * bb:128 * bb + 128],
-                              T.qz[:, a:b], T.sz[:, a:b], k, ("ldw", 32)))
-        a_z = []
-        for h in range(2):
+
+        def z_home(t):
+            k_z[1, t] = tt(T.zz[:, 4 * HC + t:4 * (HC + K):4], T.gh[:, 4 * BOTH + t:4 * HC:4], T.hd[:, t:4 * K:4],
+                           A.subtract, a_hd[t])
+
+        def layer(h):
             a, b = half(h)
-            a_z.append(act(T.z32[:, 4 * a:4 * b], T.zz[:, 4 * a:4 * b], 32.0, k_z[h]))
-            if h == 0 and r == R - 1:
-                a_od = act(T.odr[:], T.cols[:].indirect(go[:]), 1.0, k_gt, g_cols)
-                wait("sync", a_od)
-                g.sync.dma_start(T.od[:], T.odr[0:128:16, :]).then_inc(S.outs, 16)
-        k_add = []
-        for h in range(2):
+            k = quant(T.qz[:, a:b], T.sz[:, a:b], T.zz[:, 4 * a:4 * b], k_z[h, 3])
+            for t in range(4):
+                p_r[h, t] = mm(4 * h + t, HC, T.qw[:, 128 * t:128 * t + 128], T.sw[:, 128 * t:128 * t + 128],
+                               T.qz[:, a:b], T.sz[:, a:b], k, ("ldw", 32))
+
+        def times32(h):
             a, b = half(h)
-            for bb in range(4):
-                k_add.append(tt(plane(T.x32, bb, a, b), T.pp[:, (4 * h + bb) * BANK:(4 * h + bb) * BANK + HC],
-                                T.z32[:, 4 * a + bb:4 * b:4], A.add, p_r[4 * h + bb], a_z[h]))
+            for t in range(4):
+                a_z[h, t] = act(plane(T.z32, t, a, b), T.zz[:, 4 * a + t:4 * b:4], 32.0, k_z[h, t], k_both)
+
+        def add(h, t):
+            a, b = half(h)
+            k_add.append(tt(plane(T.x32, t, a, b), T.pp[:, (4 * h + t) * BANK:(4 * h + t) * BANK + HC],
+                            plane(T.z32, t, a, b), A.add, p_r[h, t], a_z[h, t]))
+
+        z_came(0)
+        tt(T.zz[:, 4 * K:4 * HC], T.gh[:, 0:4 * BOTH], T.hh[:, 4 * HC:4 * HOME], A.subtract, k_g)
+        k_both = tt(T.zz[:, 4 * (HC + K):4 * C], T.gh[:, 4 * HC:4 * HOME], T.hh[:, 0:4 * BOTH], A.subtract)
+        for t in (1, 2, 3):
+            z_came(t)
+        times32(0)
+        z_home(0)
+        layer(0)
+        for t in (1, 2, 3):
+            z_home(t)
+        times32(1)
+        add(0, 0)
+        layer(1)
+        for i in range(1, 8):
+            add(i // 4, i % 4)
         a_x = [act(T.xt[:, 4 * half(i // 4)[0] + i % 4:4 * half(i // 4)[1]:4], plane(T.x32, i % 4, *half(i // 4)),
-                   1.0 / 32, k_add[i]) for i in range(6)]
-        k_x = [[a_x[3]], [a_x[5]]]
-        late = [lambda bb=bb, k=k_add[4 + bb]: ts(T.xt[:, 4 * HC + bb:4 * C:4], plane(T.x32, bb, HC, C), 1.0 / 32,
-                                                  A.mult, k) for bb in (2, 3)]
+                   1.0 / 32, k_add[i]) for i in range(NACT)]
+        for t in range(NACT - 4, 4):
+            k = ts(T.xt[:, 4 * HC + t:4 * C:4], plane(T.x32, t, HC, C), 1.0 / 32, A.mult, k_add[4 + t])
+        k_x = [[a_x[3]], [a_x[-1], k]]
 
     g.sync.wait_ge(S.outs, 80)
     g.scalar.wait_ge(S.outa, 64)

@@ -7,7 +7,7 @@ NB = C // 32
 HOME = C - K
 BOTH = HC - K
 LH, LT = HOME // 16, K // 16
-MSG = 34
+MSG = 64
 UNIT = 4096.0
 WHOLE = 1.5 * 2 ** 23 * UNIT
 ROUND = 16 * WHOLE
@@ -30,8 +30,9 @@ SCRATCH = {
     "val": ("sbuf", [128, C], "bfloat16"), "cols": ("sbuf", [128, C], "float32"),
     "mk": ("sbuf", [128, 32], "bfloat16"), "c6": ("sbuf", [128, 64], "bfloat16"),
     "zr": ("sbuf", [128, FIVE + 32], "bfloat16"), "st": ("sbuf", [128, C], "float32"),
-    "vp": ("sbuf", [128, 64], "bfloat16"), "vtt": ("sbuf", [128, 64], "bfloat16"),
-    "own": ("sbuf", [128, 64], "float32"), "mq": ("sbuf", [128, FIVE + 32], "float32"),
+    "vp": ("sbuf", [128, 64], "bfloat16"), "cnt": ("sbuf", [128, MSG], "float32"),
+    "tv": ("sbuf", [128, 32], "float32"), "own": ("sbuf", [128, 33], "float32"), "dif": ("sbuf", [128, MSG], "float32"),
+    "mq": ("sbuf", [128, 2 * FIVE + 32], "float32"),
     "pa": ("sbuf", [128, FIVE + 32], "bfloat16"), "pb": ("sbuf", [128, FIVE], "float32"),
     "oa": ("sbuf", [128, FIVE + 32], "float32"), "ob": ("sbuf", [128, FIVE], "float32"),
     "yp": ("sbuf", [128, 96], "float32"), "mkn": ("sbuf", [128, 32], "bfloat16"),
@@ -40,7 +41,8 @@ SCRATCH = {
     "lw": ("sbuf", [128, 2 * C], "bfloat16"), "lt": ("sbuf", [128, 2 * C], "bfloat16"),
     "fo": ("sbuf", [128, 2 * NB], "float32"),
     "odr": ("sbuf", [128, C], "float32"),
-    "dd": ("sbuf", [128, 4 * C], "bfloat16"), "hd": ("sbuf", [128, 4 * K], "bfloat16"),
+    "dd": ("sbuf", [128, 4 * C], "bfloat16"), "dg": ("sbuf", [128, 4 * K], "bfloat16"),
+    "hd": ("sbuf", [128, 4 * K], "bfloat16"),
     "hh": ("sbuf", [128, 4 * HOME], "bfloat16"), "gh": ("sbuf", [128, 4 * HOME], "bfloat16"),
     "zz": ("sbuf", [128, 4 * C], "bfloat16"),
     "z32": ("sbuf", [128, 4 * C], "bfloat16"), "x32": ("sbuf", [128, 4 * C], "bfloat16"),
@@ -51,8 +53,8 @@ SCRATCH = {
 for _r in range(R):
     SCRATCH["lq%d" % _r] = ("sbuf", [128, C], "float8_e4m3fn_x4")
     SCRATCH["ls%d" % _r] = ("sbuf", [128, C], "uint8")
-    SCRATCH["cu%d" % _r] = ("sbuf", [128, 64], "float16")
-    SCRATCH["land%d" % _r] = ("sbuf", [128, TEAM * MSG], "float16")
+    SCRATCH["cu%d" % _r] = ("sbuf", [128, MSG], "bfloat16")
+    SCRATCH["land%d" % _r] = ("sbuf", [128, TEAM * MSG], "bfloat16")
     SCRATCH["go%d" % _r] = ("sbuf", [128, LH + LT], "uint16")
     SCRATCH["came%d" % _r] = ("sbuf", [128, LT], "uint16")
 for _r in range(R + 1):
@@ -60,7 +62,7 @@ for _r in range(R + 1):
     SCRATCH["sx%d" % _r] = ("sbuf", [128, C], "uint8")
 
 SEMAPHORES = (["dve", "act", "pe", "gp", "ldxa", "ldxb", "ldu", "ldw", "ldv", "outs", "outa", "sent"]
-              + [s % r for r in range(R) for s in ("varr%d", "barr%d", "larr%d")])
+              + [s % r for r in range(R) for s in ("varr%d", "narr%d", "barr%d", "carr%d", "larr%d")])
 
 
 def as_mask(engines):
@@ -70,18 +72,16 @@ def as_mask(engines):
     return m
 
 
-def vote_plan(cores, topo, rank):
+def vote_plan(cores, topo, rank, r):
     base = rank - rank % TEAM
     dsts = [d for d in range(base, base + TEAM) if d != rank]
     src = cores[rank]
     far = [d for d in dsts if topo.chip(cores[d]) != topo.chip(src)]
+    far.sort(key=lambda d: topo.chip(cores[d]) == topo.chip(cores[(d + 1) % len(cores)]))
     near = [d for d in dsts if d not in far]
     used = list(topo.engines(src, cores[far[0]]))
-    plan = [(used, far)]
-    if near:
-        free = [e for e in topo.engines(src, cores[near[0]]) if e not in used]
-        plan.append((free[:len(used) * len(near) // len(far)], near))
-    return plan
+    free = [e for e in topo.engines(src, cores[near[0]]) if e not in used]
+    return (used, far), (free, near)
 
 
 def rank_program(g, core, T, topo):
@@ -159,12 +159,15 @@ def rank_program(g, core, T, topo):
     def half(h):
         return h * HC, (h + 1) * HC
 
+    def codes(buf, h):
+        return buf[:, h * HC:(h + 1) * HC].bitcast(dt.uint8)
+
     def plane(buf, t, a=0, b=C):
         return buf[:, C * t + a:C * t + b]
 
-    g.sync.dma_start(T.x0[:, 0:4 * HC], T.x[:, 0:4 * HC]).then_inc(S.ldxa, 16)
-    g.scalar.dma_start(T.ut[:], T.u[:]).then_inc(S.ldu, 16)
-    g.sync.dma_start(T.x0[:, 4 * HC:4 * C], T.x[:, 4 * HC:4 * C]).then_inc(S.ldxb, 16)
+    g.sync.dma_start(T.x0[:, 0:4 * HOME], T.x[:, 0:4 * HOME]).then_inc(S.ldxa, 16)
+    g.sync.dma_start(T.ut[:], T.u[:]).then_inc(S.ldu, 16)
+    g.sync.dma_start(T.x0[:, 4 * HOME:4 * C], T.x[:, 4 * HOME:4 * C]).then_inc(S.ldxb, 16)
 
     def load_layer(ticket):
         wait("sync", ticket)
@@ -185,17 +188,16 @@ def rank_program(g, core, T, topo):
     k_mk = fill(T.mk[:], 1.0)
     fill(T.vp[:], 0.0)
     fill(T.c6[:, 0:32], 0.0)
-    fill(T.c6[:, 32:64], -0.5)
+    fill(T.c6[:, 32:64], -TEAM / 2)
     ts(T.pi[:, 1:2], T.pi[:, 0:1], 31, A.bitwise_and, g_pi)
     k = ts(T.pi[:, 2:3], T.pi[:, 0:1], 16, A.bitwise_and)
     fill(T.mk[:, NB - 1:NB], 0.0, k_mk)
     k_h = cpy(T.cf[:, 7:8], T.pi[:, 2:3], k)
     k = ts2(T.pi[:, 3:4], T.pi[:, 1:2], float(NB), float(-NB), A.is_ge, A.mult)
-    fill(T.et[:, 0:1024], 0.0)
+    fill(T.et[:, 0:512], 0.0)
     k = tt(T.cf[:, 0:1], T.pi[:, 1:2], T.pi[:, 3:4], A.add, k)
-    fill(T.et[:, 1024:2048], 0.0)
-    k_const = ts(T.cf[:, 1:2], T.cf[:, 0:1], -16.0, A.mult, k)
-    k_qu = quant(T.qu[:], T.su[:], T.ut[:], ("ldu", 16))
+    fill(T.et[:, 512:1024], 0.0)
+    k_const = ts2(T.cf[:, 1:2], T.cf[:, 0:1], -16.0 * TEAM, 0.25 - member / 2 - UNIT / 2, A.mult, A.add, k)
 
     def const(buf, a, b, step, c, *deps):
         return act_bias(buf[:, a:b:step], T.zr[:, 0:len(range(a, b, step))], 1.0, c, k_zr, *deps)
@@ -205,8 +207,10 @@ def rank_program(g, core, T, topo):
     a = const(T.pb, 0, FIVE, 1, 1.0)
     const(T.pa, 0, FIVE + 32, 1, 1.0)
     for o, c in ((2, WHOLE), (3, -WHOLE), (4, -UNIT)):
-        const(T.mq, o, FIVE, 5, c)
-    const(T.mq, FIVE + 1, FIVE + 32, 1, 0.0)
+        const(T.mq, FIVE + o, 2 * FIVE, 5, c)
+    const(T.mq, 2 * FIVE + 1, 2 * FIVE + 32, 1, 0.0)
+    const(T.own, 0, 1, 1, 0.0)
+    const(T.dif, 0, 32, 1, 0.0)
     const(T.pat, 0, STEPS * wide, STEPS, 0.0, a)
     const(T.pb, 0, FIVE, 5, 0.0)
     const(T.sq, 1, STEPS, 5, 0.0)
@@ -216,20 +220,19 @@ def rank_program(g, core, T, topo):
         const(T.sq, STEPS * NB * e + 4, STEPS * NB * (e + 1), STEPS, 16 * e * UNIT - ROUND)
     a = act_bias(T.cf[:, 6:7], T.cf[:, 0:1], -32.0, float(C), k_const)
     act(T.cf[:, 2:3], T.cf[:, 0:1], -32.0 * UNIT)
-    act_bias(T.mq[:, FIVE:FIVE + 1], T.cf[:, 0:1], 32.0 * UNIT, 32.0 * UNIT)
+    act_bias(T.mq[:, 2 * FIVE:2 * FIVE + 1], T.cf[:, 0:1], 32.0 * UNIT, 32.0 * UNIT)
     act(T.mkn[:], T.mk[:], -1.0)
     act_bias(T.pb[:, 4:FIVE:5], T.ii[:], -1.0, T.cf[:, 6:7], g_ii, a)
     a_val = act_bias(T.val[:], T.vi[:], 1.0, T.cf[:, 7:8], g_vi, k_h)
+    a_et = act(T.et[:, 1024:2048], T.et[:, 0:1024], 1.0)
     for t in range(4):
         a_xp = act(plane(T.x32, t), T.x0[:, t:4 * C:4], 32.0, ("ldxa", 16), ("ldxb", 16))
 
-    plans = [vote_plan(cores, topo, q) for q in range(n)]
-    arrivals = sum(len(en) for q in range(n) for en, ds in plans[q] if rank in ds)
     sent = [0]
     rid_n, pid_n = topo.addr(cores[nxt])[0:2]
 
     def bulk(src, dst):
-        return plans[src][0][0], list(topo.engines(cores[src], cores[dst]))
+        return vote_plan(cores, topo, src, 0)[0][0], list(topo.engines(cores[src], cores[dst]))
 
     def to_next(dst, src, sem, engines):
         g.remote_dma(dst, src, sem, S.sent, pid_n, rid_n, as_mask(engines))
@@ -246,18 +249,22 @@ def rank_program(g, core, T, topo):
         xt = T.x0 if r == 0 else T.xt
         qx, sx = T["qx%d" % r], T["sx%d" % r]
         k_q, p_s = [], []
-        for h in range(2):
-            a, b = half(h)
+        cut = HOME if r == 0 else HC
+        for h, (a, b) in enumerate(((0, cut), (cut, C))):
             k_q.append(quant(qx[:, a:b], sx[:, a:b], xt[:, 4 * a:4 * b], *k_x[h]))
+            if r == 0 and h == 0:
+                k_qu = quant(T.qu[:], T.su[:], T.ut[:], ("ldu", 16))
             if last:
-                p_s.append(mm(4 * h, HC, T.qv[:], T.sv[:], qx[:, a:b], sx[:, a:b], k_q[h], k_qv))
+                p_s.append(mm(4 * h, b - a, T.qv[:], T.sv[:], qx[:, a:b], sx[:, a:b], k_q[h], k_qv))
             else:
-                p_s.append(mm(4 * h, HC, T.qu[:], T.su[:], qx[:, a:b], sx[:, a:b], k_q[h], k_qu))
-            if not last and h == (0 if r == 0 and EARLY else 1):
+                p_s.append(mm(4 * h, b - a, T.qu[:], T.su[:], qx[:, a:b], sx[:, a:b], k_q[h], k_qu))
+            if not last and h == min(r, 1):
                 wait("gp", k_q[h])
                 to_next(T["ls%d" % r][:, 0:b], sx[:, 0:b], S["barr%d" % r], en_early)
         if last:
-            k_y = [cpy(T.ys[:, half(h)[0]:half(h)[1]], T.pp[:, 4 * h * BANK:4 * h * BANK + HC], p_s[h]) for h in range(2)]
+            parts = [half(0), half(1)]
+            k_y = [cpy(T.ys[:, a:b], T.pp[:, a // HC * (4 * BANK - HC) + a:a // HC * (4 * BANK - HC) + b], p_s[a // HC])
+                   for a, b in parts]
             for h in range(2):
                 a, b = half(h)
                 wait("sync", k_q[h])
@@ -265,64 +272,71 @@ def rank_program(g, core, T, topo):
             wait("act", k_q[1])
             for q in range(4):
                 g.scalar.dma_start(T.osc[4 * q:4 * q + 4, :], sx[32 * q:32 * q + 4, :]).then_inc(S.outa, 16)
-            for h in range(2):
-                a, b = half(h)
-                wait("sync", k_y[h])
+            for (a, b), k in zip(parts, k_y):
+                wait("sync", k)
                 g.sync.dma_start(T.y[:, a:b], T.ys[:, a:b]).then_inc(S.outs, 16)
             break
         cu, land, go, came = T["cu%d" % r], T["land%d" % r], T["go%d" % r], T["came%d" % r]
         lq, ls = T["lq%d" % r], T["ls%d" % r]
-        k_ta = tr(T.st[:, 0:HC], T.pp[:, 0:HC], p_s[0])
-        k = tr(T.st[:, HC:C], T.pp[:, 4 * BANK:4 * BANK + HC], p_s[1])
+        tr(T.st[:, 0:cut], T.pp[:, 0:cut], p_s[0])
+        k = tr(T.st[:, cut:C], T.pp[:, 4 * BANK:4 * BANK + C - cut], p_s[1])
         for e in range(2):
             k2 = tt(T.vp[:, 32 + NB * e:32 + NB * e + NB], T.st[:, 16 * e:C:32], T.st[:, 16 * e + 1:C:32],
                     A.is_ge, k)
         k = scan(T.vp[:, 1:2 * NB], T.vp[:, 32:32 + 2 * NB - 1], T.mk[:, 0:2 * NB - 1], 0.0, A.add, A.mult, k2)
-        k = tr(T.vtt[:], T.vp[:], k)
-        k_cu = scan(cu[:], T.vtt[:], T.c6[:], T.cf[:, 1:2], A.add, A.add, k, k_const)
+        k_cu = tr(cu[:], T.vp[:], k)
         wait("gp", k_cu)
         transfers = []
-        for en, ds in plans[rank]:
+        for sem, (en, ds) in zip(("varr%d", "narr%d"), vote_plan(cores, topo, rank, r)):
             transfers.append(RemoteDMATransfer(
                 dst_ids=[DstId(rid=topo.addr(cores[d])[0], pnc=topo.addr(cores[d])[1]) for d in ds],
-                dma_engine_mask=as_mask(en), remote_sem=S["varr%d" % r], srcs=[cu[:, 64 - MSG:64]],
+                dma_engine_mask=as_mask(en), remote_sem=S[sem % r], srcs=[cu[:]],
                 dsts=[land[:, MSG * member:MSG * member + MSG] for d in ds]))
             sent[0] += len(en)
-        g.remote_dma_fused(transfers, local_sem=S.sent)
-        to_next(lq[:].bitcast(dt.uint8), qx[:].bitcast(dt.uint8), S["barr%d" % r], en_codes)
-        if r == 0 and EARLY:
-            to_next(ls[:, HC:C], sx[:, HC:C], S["barr%d" % r], en_codes)
-        k = ts2(T.own[:, 32:64], T.vtt[:, 32:64], UNIT, 0.25 - UNIT / 2, A.mult, A.add)
+        for transfer in transfers:
+            g.remote_dma_fused([transfer], local_sem=S.sent)
+        to_next(codes(lq, 0), codes(qx, 0), S["barr%d" % r], en_codes)
+        if r == 0:
+            to_next(ls[:, cut:C], sx[:, cut:C], S.carr0, en_codes)
+        to_next(codes(lq, 1), codes(qx, 1), S["carr%d" % r], en_codes)
+        (en_far, far), (en_near, near) = vote_plan(cores, topo, rank, r)
+        upto = {m: 32 if m % TEAM < member else 31 for m in far + near}
+        scan(T.cnt[:], cu[:], T.c6[:], T.cf[:, 1:2], A.add, A.add, k_cu, k_const)
+        k = ts(T.tv[:], cu[:, 32:64], UNIT, A.mult)
         for sign in (T.pa[:, 0:FIVE:5], T.pa[:, 2:FIVE:5], T.pb[:, 2:FIVE:5]):
-            ts2(sign, T.vtt[:, 32:64], 2.0, -1.0, A.mult, A.add, a_val)
-        k_own = tt(T.own[:, 0:32], T.own[:, 32:64], cu[:, 64 - MSG + 1:64 - MSG + 33], A.add, k, k_cu)
+            ts2(sign, cu[:, 32:64], 2.0, -1.0, A.mult, A.add, a_val)
+        k = tt(T.own[:, 1:33], T.cnt[:, 31:63], T.tv[:], A.add, k)
         fill(T.lw[:], float(HC))
+        k_own = tt(T.dif[:, upto[near[0]]:upto[near[0]] + 32], T.own[:, 1:33], T.own[:, 0:32], A.subtract, k)
         if r == 0:
             for b in range(4):
-                k_et = cpy(T.et[:, 512 * b + b:512 * b + 512:4], T.ident[:], g_id)
+                k_et = cpy(T.et[:, 512 * b + b:512 * b + 512:4], T.ident[:], g_id, a_et)
             k_qe = quant(T.qe[:], T.se[:], T.et[:], k_et)
             wait("dve", a_xp)
-            if WLATE:
-                load_layer(("varr0", arrivals))
         if r == 1:
             k_qv = quant(T.qv[:], T.sv[:], T.vt[:], ("ldv", 16))
         if r == R - 1:
             g_cols = done("gp", g.iota(T.cols[:], [[1, C]], 0, 0, allow_small_or_imprecise_dtypes=True))
-        a_d = None
-        for b in range(4):
-            p = mm(b, C, T.qe[:, 128 * b:128 * b + 128], T.se[:, 128 * b:128 * b + 128], lq[:], ls[:],
-                   ("barr%d" % r, in_early + (2 if r == 0 and EARLY else 1) * in_codes), k_qe, k_ta)
-            a_d = act(plane(T.dd, b), T.pp[:, b * BANK:b * BANK + C], 1.0, p)
+        landed = [("barr%d" % r, in_early + in_codes), ("carr%d" % r, (2 if r == 0 else 1) * in_codes)]
+        for h in range(2):
+            a, b = half(h)
+            for t in range(4):
+                p = mm(4 * h + t, HC, T.qe[:, 128 * t:128 * t + 128], T.se[:, 128 * t:128 * t + 128],
+                       lq[:, a:b], ls[:, a:b], landed[h], k_qe, k_cu)
+                a_d = act(plane(T.dd, t, a, b), T.pp[:, (4 * h + t) * BANK:(4 * h + t) * BANK + HC], 1.0, p)
 
         def term(m):
-            o = 2 if m < member else 1
-            return land[:, MSG * m + o:MSG * m + o + 32]
+            return land[:, MSG * (m % TEAM):MSG * (m % TEAM) + upto[m] + 32]
 
-        mates = [m for m in range(TEAM) if m != member]
-        tt(T.mq[:, 0:FIVE:5], T.own[:, 0:32], term(mates[0]), A.add, ("varr%d" % r, arrivals), k_own)
-        k = tt(T.mq[:, 1:FIVE:5], term(mates[1]), term(mates[2]), A.add)
-        k = scan(T.oa[:], T.pa[:], T.mq[:], T.cf[:, 2:3], A.mult, A.add, k)
-        k2 = scan(T.ob[:], T.pb[:], T.mq[:, 0:FIVE], 0.0, A.mult, A.add)
+        def slot(m, o):
+            a = FIVE - 5 * upto[m] + o
+            return T.mq[:, a:a + 5 * (upto[m] + 32):5]
+
+        scan(slot(near[0], 0), term(near[0]), T.dif[:, 0:upto[near[0]] + 32], 0.0, A.add, A.add,
+             ("narr%d" % r, len(en_near)), k_own)
+        k = scan(slot(far[0], 1), term(far[0]), term(far[1]), 0.0, A.add, A.add, ("varr%d" % r, 2 * len(en_far)))
+        k = scan(T.oa[:], T.pa[:], T.mq[:, FIVE:2 * FIVE + 32], T.cf[:, 2:3], A.mult, A.add, k)
+        k2 = scan(T.ob[:], T.pb[:], T.mq[:, FIVE:2 * FIVE], 0.0, A.mult, A.add)
         k = tr(T.yp[:, 64:96], T.oa[:, FIVE:FIVE + 32], k)
         tr(T.yp[:, 32:64], T.oa[:, 4:FIVE:5])
         k2 = tr(T.yp[:, 0:32], T.ob[:, 4:FIVE:5], k2)
@@ -344,22 +358,29 @@ def rank_program(g, core, T, topo):
         to_next(came[:], go[:, LH:LH + LT], S["larr%d" % r], en_codes)
         k_h = [ts(T.hh[:, t:4 * HOME:4], plane(T.x32, t).indirect(go[:, 0:LH]), 1.0 / 64, A.mult, k_gh) for t in (0, 1)]
         k_h += [act(T.hh[:, t:4 * HOME:4], plane(T.x32, t).indirect(go[:, 0:LH]), 1.0 / 64, k_gh) for t in (2, 3)]
-        if r == R - 1:
-            a_od = act(T.odr[:], T.cols[:].indirect(go[:]), 1.0, g_cols)
-            wait("sync", a_od)
-            g.sync.dma_start(T.od[:], T.odr[0:128:16, :]).then_inc(S.outs, 16)
-        for t in (0, 2, 1, 3):
-            k_g = ts(T.gh[:, t:4 * HOME:4], T.hh[:, t:4 * HOME:4], 2.0, A.mult, k_h[t])
+        def twice(a, b, step, *deps):
+            return ts(T.gh[:, a:b:step], T.hh[:, a:b:step], 2.0, A.mult, *deps)
+
+        for t in (2, 3):
+            act(T.gh[:, 4 * BOTH + t:4 * HC:4], T.hh[:, 4 * BOTH + t:4 * HC:4], 2.0, k_h[t])
+        twice(4 * BOTH, 4 * HC, 4, k_h[0])
+        k = twice(0, 4 * BOTH, 1, k_h[1], k_h[3])
+        k2 = twice(4 * HC, 4 * HOME, 1)
+        twice(4 * BOTH + 1, 4 * HC, 4)
+        tt(T.zz[:, 4 * K:4 * HC], T.gh[:, 0:4 * BOTH], T.hh[:, 4 * HC:4 * HOME], A.subtract, k)
+        k_both = tt(T.zz[:, 4 * (HC + K):4 * C], T.gh[:, 4 * HC:4 * HOME], T.hh[:, 0:4 * BOTH], A.subtract, k2)
         listed = ("larr%d" % r, in_codes)
         if r == 0:
             wait("sync", listed)
             g.sync.dma_start(T.vt[:], T.v[:]).then_inc(S.ldv, 16)
-        a_hd = [act(T.hd[:, t:4 * K:4], plane(T.dd, t).indirect(came[:]), 0.5, listed, a_d) for t in range(4)]
+        a_dg = {t: act(T.dg[:, t:4 * K:4], plane(T.dd, t).indirect(came[:]), 1.0, listed, a_d) for t in (2, 3)}
+        a_hd = {t: act(T.hd[:, t:4 * K:4], plane(T.dd, t).indirect(came[:]), 0.5) for t in (0, 1)}
         k_z, a_z, p_r, k_add = {}, {}, {}, []
 
         def z_came(t):
-            k_z[0, t] = tt(T.zz[:, t:4 * K:4], plane(T.dd, t).indirect(came[:]), T.hh[:, 4 * BOTH + t:4 * HC:4],
-                           A.subtract, listed, a_d)
+            picked = T.dg[:, t:4 * K:4] if t in a_dg else plane(T.dd, t).indirect(came[:])
+            k_z[0, t] = tt(T.zz[:, t:4 * K:4], picked, T.hh[:, 4 * BOTH + t:4 * HC:4], A.subtract,
+                           listed, a_dg.get(t, a_d))
 
         def z_home(t):
             k_z[1, t] = tt(T.zz[:, 4 * HC + t:4 * (HC + K):4], T.gh[:, 4 * BOTH + t:4 * HC:4], T.hd[:, t:4 * K:4],
@@ -367,44 +388,49 @@ def rank_program(g, core, T, topo):
 
         def layer(h):
             a, b = half(h)
-            k = quant(T.qz[:, a:b], T.sz[:, a:b], T.zz[:, 4 * a:4 * b], k_z[h, 3])
+            k = quant(T.qz[:, a:b], T.sz[:, a:b], T.zz[:, 4 * a:4 * b], *[k_z[h, t] for t in range(4)])
             for t in range(4):
                 p_r[h, t] = mm(4 * h + t, HC, T.qw[:, 128 * t:128 * t + 128], T.sw[:, 128 * t:128 * t + 128],
                                T.qz[:, a:b], T.sz[:, a:b], k, ("ldw", 32))
 
         def times32(h):
-            a, b = half(h)
-            for t in range(4):
-                a_z[h, t] = act(plane(T.z32, t, a, b), T.zz[:, 4 * a + t:4 * b:4], 32.0, k_z[h, t], k_both)
+            if h == 0:
+                for t in range(4):
+                    a_z[h, t] = act(T.z32[:, t:4 * HC:4], T.zz[:, t:4 * HC:4], 32.0, k_z[h, t])
+            else:
+                k = act(T.z32[:, 4 * HC:4 * (HC + K)], T.zz[:, 4 * HC:4 * (HC + K)], 32.0, k_z[h, 1])
+                a_z.update({(h, t): k for t in range(4)})
 
         def add(h, t):
             a, b = half(h)
             k_add.append(tt(plane(T.x32, t, a, b), T.pp[:, (4 * h + t) * BANK:(4 * h + t) * BANK + HC],
-                            plane(T.z32, t, a, b), A.add, p_r[h, t], a_z[h, t]))
+                            T.z32[:, 4 * a + t:4 * b:4], A.add, p_r[h, t], a_z[h, t]))
 
-        z_came(0)
-        tt(T.zz[:, 4 * K:4 * HC], T.gh[:, 0:4 * BOTH], T.hh[:, 4 * HC:4 * HOME], A.subtract, k_g)
-        k_both = tt(T.zz[:, 4 * (HC + K):4 * C], T.gh[:, 4 * HC:4 * HOME], T.hh[:, 0:4 * BOTH], A.subtract)
-        for t in (1, 2, 3):
+        for t in range(4):
             z_came(t)
         times32(0)
-        z_home(0)
+        for t in a_dg:
+            a_hd[t] = ts(T.hd[:, t:4 * K:4], T.dg[:, t:4 * K:4], 0.5, A.mult)
         layer(0)
-        for t in (1, 2, 3):
+        for t in (2, 3, 0, 1):
             z_home(t)
+        ts(T.z32[:, 4 * (HC + K):4 * C], T.zz[:, 4 * (HC + K):4 * C], 32.0, A.mult, k_both)
         times32(1)
-        add(0, 0)
         layer(1)
-        for i in range(1, 8):
+        for i in range(8):
             add(i // 4, i % 4)
         a_x = [act(T.xt[:, 4 * half(i // 4)[0] + i % 4:4 * half(i // 4)[1]:4], plane(T.x32, i % 4, *half(i // 4)),
                    1.0 / 32, k_add[i]) for i in range(NACT)]
         for t in range(NACT - 4, 4):
             k = ts(T.xt[:, 4 * HC + t:4 * C:4], plane(T.x32, t, HC, C), 1.0 / 32, A.mult, k_add[4 + t])
         k_x = [[a_x[3]], [a_x[-1], k]]
+        if r == R - 1:
+            a_od = act(T.odr[:], T.cols[:].indirect(go[:]), 1.0, g_cols)
+            wait("act", a_od)
+            g.scalar.dma_start(T.od[:], T.odr[0:128:16, :]).then_inc(S.outa, 16)
 
-    g.sync.wait_ge(S.outs, 80)
-    g.scalar.wait_ge(S.outa, 64)
+    g.sync.wait_ge(S.outs, 64)
+    g.scalar.wait_ge(S.outa, 80)
     g.wait_ge(S.sent, sent[0])
     for q in ("dve", "act", "pe", "gp"):
         wait("gp", (q, count[q]))

from concourse.bass import DstId, RemoteDMATransfer
from concourse.mybir import dt, AluOpType, ActivationFunctionType

C, K, R, TEAM = 320, 128, 3, 4
HC = C // 2
NB = C // 32
HOME = C - K
BOTH = HC - K
LH, LT = HOME // 16, K // 16
MSG = 64
UNIT = 4096.0
WHOLE = 1.5 * 2 ** 23 * UNIT
ROUND = 16 * WHOLE
FIVE = 5 * 32
STEPS = 7
BANK = 512
EARLY, NACT, WLATE = True, 5, False

SCRATCH = {
    "x0": ("sbuf", [128, 4 * C], "bfloat16"), "xt": ("sbuf", [128, 4 * C], "bfloat16"),
    "ut": ("sbuf", [128, 512], "bfloat16"), "vt": ("sbuf", [128, 512], "bfloat16"),
    "qu": ("sbuf", [128, 128], "float8_e4m3fn_x4"), "su": ("sbuf", [128, 128], "uint8"),
    "qv": ("sbuf", [128, 128], "float8_e4m3fn_x4"), "sv": ("sbuf", [128, 128], "uint8"),
    "qw": ("sbuf", [128, 512], "float8_e4m3fn_x4"), "sw": ("sbuf", [128, 512], "uint8"),
    "one128": ("sbuf", [128, 128], "bfloat16"), "ident": ("sbuf", [128, 128], "bfloat16"),
    "et": ("sbuf", [128, 2048], "bfloat16"),
    "qe": ("sbuf", [128, 512], "float8_e4m3fn_x4"), "se": ("sbuf", [128, 512], "uint8"),
    "pi": ("sbuf", [128, 4], "int32"), "cf": ("sbuf", [128, 16], "float32"),
    "ii": ("sbuf", [128, 32], "float32"), "vi": ("sbuf", [128, C], "float32"),
    "val": ("sbuf", [128, C], "bfloat16"), "cols": ("sbuf", [128, C], "float32"),
    "mk": ("sbuf", [128, 32], "bfloat16"), "c6": ("sbuf", [128, 64], "bfloat16"),
    "zr": ("sbuf", [128, FIVE + 32], "bfloat16"), "st": ("sbuf", [128, C], "float32"),
    "vp": ("sbuf", [128, 64], "bfloat16"), "cnt": ("sbuf", [128, MSG], "float32"),
    "tv": ("sbuf", [128, 32], "float32"), "own": ("sbuf", [128, 33], "float32"), "dif": ("sbuf", [128, MSG], "float32"),
    "mq": ("sbuf", [128, 2 * FIVE + 32], "float32"),
    "pa": ("sbuf", [128, FIVE + 32], "bfloat16"), "pb": ("sbuf", [128, FIVE], "float32"),
    "oa": ("sbuf", [128, FIVE + 32], "float32"), "ob": ("sbuf", [128, FIVE], "float32"),
    "yp": ("sbuf", [128, 96], "float32"), "mkn": ("sbuf", [128, 32], "bfloat16"),
    "sq": ("sbuf", [128, STEPS * 2 * NB], "float32"), "so": ("sbuf", [128, STEPS * 2 * NB], "float32"),
    "pat": ("sbuf", [128, STEPS * 2 * NB], "float32"), "offs": ("sbuf", [128, 2 * NB], "uint16"),
    "lw": ("sbuf", [128, 2 * C], "bfloat16"), "lt": ("sbuf", [128, 2 * C], "bfloat16"),
    "fo": ("sbuf", [128, 2 * NB], "float32"),
    "odr": ("sbuf", [128, C], "float32"),
    "dd": ("sbuf", [128, 4 * C], "bfloat16"), "dg": ("sbuf", [128, 4 * K], "bfloat16"),
    "hd": ("sbuf", [128, 4 * K], "bfloat16"),
    "hh": ("sbuf", [128, 4 * HOME], "bfloat16"), "gh": ("sbuf", [128, 4 * HOME], "bfloat16"),
    "zz": ("sbuf", [128, 4 * C], "bfloat16"),
    "z32": ("sbuf", [128, 4 * C], "bfloat16"), "x32": ("sbuf", [128, 4 * C], "bfloat16"),
    "qz": ("sbuf", [128, C], "float8_e4m3fn_x4"), "sz": ("sbuf", [128, C], "uint8"),
    "ys": ("sbuf", [128, C], "float32"),
    "pp": ("psum", [128, 8 * BANK], "float32"),
}
for _r in range(R):
    SCRATCH["lq%d" % _r] = ("sbuf", [128, C], "float8_e4m3fn_x4")
    SCRATCH["ls%d" % _r] = ("sbuf", [128, C], "uint8")
    SCRATCH["cu%d" % _r] = ("sbuf", [128, MSG], "bfloat16")
    SCRATCH["land%d" % _r] = ("sbuf", [128, TEAM * MSG], "bfloat16")
    SCRATCH["go%d" % _r] = ("sbuf", [128, LH + LT], "uint16")
    SCRATCH["came%d" % _r] = ("sbuf", [128, LT], "uint16")
for _r in range(R + 1):
    SCRATCH["qx%d" % _r] = ("sbuf", [128, C], "float8_e4m3fn_x4")
    SCRATCH["sx%d" % _r] = ("sbuf", [128, C], "uint8")

SEMAPHORES = (["dve", "act", "pe", "gp", "ldxa", "ldxb", "ldu", "ldw", "ldv", "outs", "outa", "sent"]
              + [s % r for r in range(R) for s in ("varr%d", "narr%d", "barr%d", "carr%d", "larr%d")])


def as_mask(engines):
    m = 0
    for e in engines:
        m |= 1 << e
    return m


def vote_plan(cores, topo, rank, r):
    base = rank - rank % TEAM
    dsts = [d for d in range(base, base + TEAM) if d != rank]
    src = cores[rank]
    far = [d for d in dsts if topo.chip(cores[d]) != topo.chip(src)]
    far.sort(key=lambda d: topo.chip(cores[d]) == topo.chip(cores[(d + 1) % len(cores)]))
    near = [d for d in dsts if d not in far]
    used = list(topo.engines(src, cores[far[0]]))
    free = [e for e in topo.engines(src, cores[near[0]]) if e not in used]
    return (used, far), (free, near)


def rank_program(g, core, T, topo):
    rank = T.rank_of(core)
    if rank is None:
        return
    cores = list(T.cores)
    n = len(cores)
    A = AluOpType
    COPY, IDENT = ActivationFunctionType.Copy, ActivationFunctionType.Identity
    S = T.sem
    V, ACT, PE = g.vector, g.scalar, g.tensor
    member = rank % TEAM
    prev, nxt = (rank - 1) % n, (rank + 1) % n

    queues = {"dve": V, "act": ACT, "pe": PE, "gp": g, "sync": g.sync}
    count = {"dve": 0, "act": 0, "pe": 0, "gp": 0}
    waited = {}

    def wait(q, *tickets):
        for name, val in tickets:
            if waited.get((q, name), 0) < val:
                queues[q].wait_ge(S[name], val)
                waited[(q, name)] = val

    def done(q, ins):
        count[q] += 1
        ins.then_inc(S[q], 1)
        return (q, count[q])

    def tt(out, a, b, op, *deps):
        wait("dve", *deps)
        return done("dve", V.tensor_tensor(out, a, b, op))

    def ts(out, a, s1, op0, *deps):
        wait("dve", *deps)
        return done("dve", V.tensor_scalar(out, a, s1, None, op0))

    def ts2(out, a, s1, s2, op0, op1, *deps):
        wait("dve", *deps)
        return done("dve", V.tensor_scalar(out, a, s1, s2, op0, op1))

    def scan(out, d0, d1, init, op0, op1, *deps):
        wait("dve", *deps)
        return done("dve", V.tensor_tensor_scan(out, d0, d1, init, op0, op1))

    def tr(out, a, *deps):
        wait("dve", *deps)
        return done("dve", V.transpose(out, a))

    def cpy(out, a, *deps):
        wait("dve", *deps)
        return done("dve", V.tensor_copy(out, a))

    def fill(out, c, *deps):
        wait("dve", *deps)
        return done("dve", V.memset(out, c))

    def quant(q, s, a, *deps):
        wait("dve", *deps)
        return done("dve", V.quantize_mx(q, s, a))

    def act(out, a, scale, *deps):
        wait("act", *deps)
        return done("act", ACT.activation(out, a, COPY, scale=scale))

    def act_bias(out, a, scale, bias, *deps):
        wait("act", *deps)
        return done("act", ACT.activation(out, a, IDENT, bias=bias, scale=scale))

    def mm(bank, cols, lq, ls, rq, rs, *deps):
        wait("pe", *deps)
        return done("pe", PE.matmul_mx(T.pp[:, bank * BANK:bank * BANK + cols], lq, ls, rq, rs, True, True))

    def half(h):
        return h * HC, (h + 1) * HC

    def codes(buf, h):
        return buf[:, h * HC:(h + 1) * HC].bitcast(dt.uint8)

    def plane(buf, t, a=0, b=C):
        return buf[:, C * t + a:C * t + b]

    g.sync.dma_start(T.x0[:, 0:4 * HOME], T.x[:, 0:4 * HOME]).then_inc(S.ldxa, 16)
    g.sync.dma_start(T.ut[:], T.u[:]).then_inc(S.ldu, 16)
    g.sync.dma_start(T.x0[:, 4 * HOME:4 * C], T.x[:, 4 * HOME:4 * C]).then_inc(S.ldxb, 16)

    def load_layer(ticket):
        wait("sync", ticket)
        g.sync.dma_start(T.qw[:].bitcast(dt.uint8), T.wc[:]).then_inc(S.ldw, 16)
        g.sync.dma_start(T.sw[:], T.ws[:]).then_inc(S.ldw, 16)

    if not WLATE:
        load_layer(("ldxa", 16))

    g_pi = done("gp", g.iota(T.pi[:, 0:1], [[0, 1]], 0, 1))
    g_ii = done("gp", g.iota(T.ii[:], [[1, 32]], 0, 0, allow_small_or_imprecise_dtypes=True))
    k_one = fill(T.one128[:], 1.0)
    wait("gp", k_one)
    g_id = done("gp", g.affine_select(T.ident[:], T.one128[:], [[-1, 128]], A.is_equal, 0.0, 0, 1))
    g_vi = done("gp", g.iota(T.vi[:], [[0, 2], [32, NB], [1, 16]], -HC, 0, allow_small_or_imprecise_dtypes=True))

    k_zr = fill(T.zr[:], 0.0)
    k_mk = fill(T.mk[:], 1.0)
    fill(T.vp[:], 0.0)
    fill(T.c6[:, 0:32], 0.0)
    fill(T.c6[:, 32:64], -TEAM / 2)
    ts(T.pi[:, 1:2], T.pi[:, 0:1], 31, A.bitwise_and, g_pi)
    k = ts(T.pi[:, 2:3], T.pi[:, 0:1], 16, A.bitwise_and)
    fill(T.mk[:, NB - 1:NB], 0.0, k_mk)
    k_h = cpy(T.cf[:, 7:8], T.pi[:, 2:3], k)
    k = ts2(T.pi[:, 3:4], T.pi[:, 1:2], float(NB), float(-NB), A.is_ge, A.mult)
    fill(T.et[:, 0:512], 0.0)
    k = tt(T.cf[:, 0:1], T.pi[:, 1:2], T.pi[:, 3:4], A.add, k)
    fill(T.et[:, 512:1024], 0.0)
    k_const = ts2(T.cf[:, 1:2], T.cf[:, 0:1], -16.0 * TEAM, 0.25 - member / 2 - UNIT / 2, A.mult, A.add, k)

    def const(buf, a, b, step, c, *deps):
        return act_bias(buf[:, a:b:step], T.zr[:, 0:len(range(a, b, step))], 1.0, c, k_zr, *deps)

    wide = 2 * NB
    a = const(T.pat, 0, STEPS * wide, 1, 1.0)
    a = const(T.pb, 0, FIVE, 1, 1.0)
    const(T.pa, 0, FIVE + 32, 1, 1.0)
    for o, c in ((2, WHOLE), (3, -WHOLE), (4, -UNIT)):
        const(T.mq, FIVE + o, 2 * FIVE, 5, c)
    const(T.mq, 2 * FIVE + 1, 2 * FIVE + 32, 1, 0.0)
    const(T.own, 0, 1, 1, 0.0)
    const(T.dif, 0, 32, 1, 0.0)
    const(T.pat, 0, STEPS * wide, STEPS, 0.0, a)
    const(T.pb, 0, FIVE, 5, 0.0)
    const(T.sq, 1, STEPS, 5, 0.0)
    const(T.sq, 2, STEPS * wide, STEPS, -7.5 * UNIT)
    const(T.sq, 3, STEPS * wide, STEPS, ROUND)
    for e in range(2):
        const(T.sq, STEPS * NB * e + 4, STEPS * NB * (e + 1), STEPS, 16 * e * UNIT - ROUND)
    a = act_bias(T.cf[:, 6:7], T.cf[:, 0:1], -32.0, float(C), k_const)
    act(T.cf[:, 2:3], T.cf[:, 0:1], -32.0 * UNIT)
    act_bias(T.mq[:, 2 * FIVE:2 * FIVE + 1], T.cf[:, 0:1], 32.0 * UNIT, 32.0 * UNIT)
    act(T.mkn[:], T.mk[:], -1.0)
    act_bias(T.pb[:, 4:FIVE:5], T.ii[:], -1.0, T.cf[:, 6:7], g_ii, a)
    a_val = act_bias(T.val[:], T.vi[:], 1.0, T.cf[:, 7:8], g_vi, k_h)
    a_et = act(T.et[:, 1024:2048], T.et[:, 0:1024], 1.0)
    for t in range(4):
        a_xp = act(plane(T.x32, t), T.x0[:, t:4 * C:4], 32.0, ("ldxa", 16), ("ldxb", 16))

    sent = [0]
    rid_n, pid_n = topo.addr(cores[nxt])[0:2]

    def bulk(src, dst):
        return vote_plan(cores, topo, src, 0)[0][0], list(topo.engines(cores[src], cores[dst]))

    def to_next(dst, src, sem, engines):
        g.remote_dma(dst, src, sem, S.sent, pid_n, rid_n, as_mask(engines))
        sent[0] += len(engines)

    en_early, en_codes = bulk(rank, nxt)
    in_early, in_codes = [len(e) for e in bulk(prev, rank)]

    k_x = [[("ldxa", 16)], [("ldxb", 16)]]
    k_qe = None
    k_qv = None
    for r in range(R + 1):
        last = r == R
        xt = T.x0 if r == 0 else T.xt
        qx, sx = T["qx%d" % r], T["sx%d" % r]
        k_q, p_s = [], []
        cut = HOME if r == 0 else HC
        for h, (a, b) in enumerate(((0, cut), (cut, C))):
            k_q.append(quant(qx[:, a:b], sx[:, a:b], xt[:, 4 * a:4 * b], *k_x[h]))
            if r == 0 and h == 0:
                k_qu = quant(T.qu[:], T.su[:], T.ut[:], ("ldu", 16))
            if last:
                p_s.append(mm(4 * h, b - a, T.qv[:], T.sv[:], qx[:, a:b], sx[:, a:b], k_q[h], k_qv))
            else:
                p_s.append(mm(4 * h, b - a, T.qu[:], T.su[:], qx[:, a:b], sx[:, a:b], k_q[h], k_qu))
            if not last and h == min(r, 1):
                wait("gp", k_q[h])
                to_next(T["ls%d" % r][:, 0:b], sx[:, 0:b], S["barr%d" % r], en_early)
        if last:
            parts = [half(0), half(1)]
            k_y = [cpy(T.ys[:, a:b], T.pp[:, a // HC * (4 * BANK - HC) + a:a // HC * (4 * BANK - HC) + b], p_s[a // HC])
                   for a, b in parts]
            for h in range(2):
                a, b = half(h)
                wait("sync", k_q[h])
                g.sync.dma_start(T.oc[:, 4 * a:4 * b], qx[:, a:b].bitcast(dt.uint8)).then_inc(S.outs, 16)
            wait("act", k_q[1])
            for q in range(4):
                g.scalar.dma_start(T.osc[4 * q:4 * q + 4, :], sx[32 * q:32 * q + 4, :]).then_inc(S.outa, 16)
            for (a, b), k in zip(parts, k_y):
                wait("sync", k)
                g.sync.dma_start(T.y[:, a:b], T.ys[:, a:b]).then_inc(S.outs, 16)
            break
        cu, land, go, came = T["cu%d" % r], T["land%d" % r], T["go%d" % r], T["came%d" % r]
        lq, ls = T["lq%d" % r], T["ls%d" % r]
        tr(T.st[:, 0:cut], T.pp[:, 0:cut], p_s[0])
        k = tr(T.st[:, cut:C], T.pp[:, 4 * BANK:4 * BANK + C - cut], p_s[1])
        for e in range(2):
            k2 = tt(T.vp[:, 32 + NB * e:32 + NB * e + NB], T.st[:, 16 * e:C:32], T.st[:, 16 * e + 1:C:32],
                    A.is_ge, k)
        k = scan(T.vp[:, 1:2 * NB], T.vp[:, 32:32 + 2 * NB - 1], T.mk[:, 0:2 * NB - 1], 0.0, A.add, A.mult, k2)
        k_cu = tr(cu[:], T.vp[:], k)
        wait("gp", k_cu)
        transfers = []
        for sem, (en, ds) in zip(("varr%d", "narr%d"), vote_plan(cores, topo, rank, r)):
            transfers.append(RemoteDMATransfer(
                dst_ids=[DstId(rid=topo.addr(cores[d])[0], pnc=topo.addr(cores[d])[1]) for d in ds],
                dma_engine_mask=as_mask(en), remote_sem=S[sem % r], srcs=[cu[:]],
                dsts=[land[:, MSG * member:MSG * member + MSG] for d in ds]))
            sent[0] += len(en)
        for transfer in transfers:
            g.remote_dma_fused([transfer], local_sem=S.sent)
        to_next(codes(lq, 0), codes(qx, 0), S["barr%d" % r], en_codes)
        if r == 0:
            to_next(ls[:, cut:C], sx[:, cut:C], S.carr0, en_codes)
        to_next(codes(lq, 1), codes(qx, 1), S["carr%d" % r], en_codes)
        (en_far, far), (en_near, near) = vote_plan(cores, topo, rank, r)
        upto = {m: 32 if m % TEAM < member else 31 for m in far + near}
        scan(T.cnt[:], cu[:], T.c6[:], T.cf[:, 1:2], A.add, A.add, k_cu, k_const)
        k = ts(T.tv[:], cu[:, 32:64], UNIT, A.mult)
        for sign in (T.pa[:, 0:FIVE:5], T.pa[:, 2:FIVE:5], T.pb[:, 2:FIVE:5]):
            ts2(sign, cu[:, 32:64], 2.0, -1.0, A.mult, A.add, a_val)
        k = tt(T.own[:, 1:33], T.cnt[:, 31:63], T.tv[:], A.add, k)
        fill(T.lw[:], float(HC))
        k_own = tt(T.dif[:, upto[near[0]]:upto[near[0]] + 32], T.own[:, 1:33], T.own[:, 0:32], A.subtract, k)
        if r == 0:
            for b in range(4):
                k_et = cpy(T.et[:, 512 * b + b:512 * b + 512:4], T.ident[:], g_id, a_et)
            k_qe = quant(T.qe[:], T.se[:], T.et[:], k_et)
            wait("dve", a_xp)
        if r == 1:
            k_qv = quant(T.qv[:], T.sv[:], T.vt[:], ("ldv", 16))
        if r == R - 1:
            g_cols = done("gp", g.iota(T.cols[:], [[1, C]], 0, 0, allow_small_or_imprecise_dtypes=True))
        landed = [("barr%d" % r, in_early + in_codes), ("carr%d" % r, (2 if r == 0 else 1) * in_codes)]
        for h in range(2):
            a, b = half(h)
            for t in range(4):
                p = mm(4 * h + t, HC, T.qe[:, 128 * t:128 * t + 128], T.se[:, 128 * t:128 * t + 128],
                       lq[:, a:b], ls[:, a:b], landed[h], k_qe, k_cu)
                a_d = act(plane(T.dd, t, a, b), T.pp[:, (4 * h + t) * BANK:(4 * h + t) * BANK + HC], 1.0, p)

        def term(m):
            return land[:, MSG * (m % TEAM):MSG * (m % TEAM) + upto[m] + 32]

        def slot(m, o):
            a = FIVE - 5 * upto[m] + o
            return T.mq[:, a:a + 5 * (upto[m] + 32):5]

        scan(slot(near[0], 0), term(near[0]), T.dif[:, 0:upto[near[0]] + 32], 0.0, A.add, A.add,
             ("narr%d" % r, len(en_near)), k_own)
        k = scan(slot(far[0], 1), term(far[0]), term(far[1]), 0.0, A.add, A.add, ("varr%d" % r, 2 * len(en_far)))
        k = scan(T.oa[:], T.pa[:], T.mq[:, FIVE:2 * FIVE + 32], T.cf[:, 2:3], A.mult, A.add, k)
        k2 = scan(T.ob[:], T.pb[:], T.mq[:, FIVE:2 * FIVE], 0.0, A.mult, A.add)
        k = tr(T.yp[:, 64:96], T.oa[:, FIVE:FIVE + 32], k)
        tr(T.yp[:, 32:64], T.oa[:, 4:FIVE:5])
        k2 = tr(T.yp[:, 0:32], T.ob[:, 4:FIVE:5], k2)
        for o in (1, 6):
            scan(T.sq[:, STEPS + o:STEPS * wide:STEPS], T.yp[:, 64:64 + wide - 1], T.mkn[:, 0:wide - 1], 0.0,
                 A.subtract, A.mult, k)
        for o in (0, 5):
            k = tt(T.sq[:, o:STEPS * wide:STEPS], T.yp[:, 0:wide], T.yp[:, 32:32 + wide], A.subtract, k2)
        k = scan(T.so[:], T.pat[:], T.sq[:], 0.0, A.mult, A.add, k)
        k = ts(T.offs[:], T.so[:, STEPS - 1:STEPS * wide:STEPS], 1.0 / UNIT, A.mult, k)
        k = cpy(T.lw[:].indirect(T.offs[:]), T.val[:], k)
        k = tr(T.lt[:, 32 * LH:2 * C], T.lw[:, 32 * LH:2 * C], k)
        k2 = tr(T.lt[:, 0:32 * LH], T.lw[:, 0:32 * LH])
        k = tt(T.fo[:, LH:LH + LT], T.lt[:, 32 * LH:2 * C:32], T.lt[:, 32 * LH + 16:2 * C:32], A.add, k)
        k2 = tt(T.fo[:, 0:LH], T.lt[:, 0:32 * LH:32], T.lt[:, 16:32 * LH:32], A.add, k2)
        k_gt = cpy(go[:, LH:LH + LT], T.fo[:, LH:LH + LT], k)
        k_gh = cpy(go[:, 0:LH], T.fo[:, 0:LH], k2)
        wait("gp", k_gt)
        to_next(came[:], go[:, LH:LH + LT], S["larr%d" % r], en_codes)
        k_h = [ts(T.hh[:, t:4 * HOME:4], plane(T.x32, t).indirect(go[:, 0:LH]), 1.0 / 64, A.mult, k_gh) for t in (0, 1)]
        k_h += [act(T.hh[:, t:4 * HOME:4], plane(T.x32, t).indirect(go[:, 0:LH]), 1.0 / 64, k_gh) for t in (2, 3)]
        def twice(a, b, step, *deps):
            return ts(T.gh[:, a:b:step], T.hh[:, a:b:step], 2.0, A.mult, *deps)

        for t in (2, 3):
            act(T.gh[:, 4 * BOTH + t:4 * HC:4], T.hh[:, 4 * BOTH + t:4 * HC:4], 2.0, k_h[t])
        twice(4 * BOTH, 4 * HC, 4, k_h[0])
        k = twice(0, 4 * BOTH, 1, k_h[1], k_h[3])
        k2 = twice(4 * HC, 4 * HOME, 1)
        twice(4 * BOTH + 1, 4 * HC, 4)
        tt(T.zz[:, 4 * K:4 * HC], T.gh[:, 0:4 * BOTH], T.hh[:, 4 * HC:4 * HOME], A.subtract, k)
        k_both = tt(T.zz[:, 4 * (HC + K):4 * C], T.gh[:, 4 * HC:4 * HOME], T.hh[:, 0:4 * BOTH], A.subtract, k2)
        listed = ("larr%d" % r, in_codes)
        if r == 0:
            wait("sync", listed)
            g.sync.dma_start(T.vt[:], T.v[:]).then_inc(S.ldv, 16)
        a_dg = {t: act(T.dg[:, t:4 * K:4], plane(T.dd, t).indirect(came[:]), 1.0, listed, a_d) for t in (2, 3)}
        a_hd = {t: act(T.hd[:, t:4 * K:4], plane(T.dd, t).indirect(came[:]), 0.5) for t in (0, 1)}
        k_z, a_z, p_r, k_add = {}, {}, {}, []

        def z_came(t):
            picked = T.dg[:, t:4 * K:4] if t in a_dg else plane(T.dd, t).indirect(came[:])
            k_z[0, t] = tt(T.zz[:, t:4 * K:4], picked, T.hh[:, 4 * BOTH + t:4 * HC:4], A.subtract,
                           listed, a_dg.get(t, a_d))

        def z_home(t):
            k_z[1, t] = tt(T.zz[:, 4 * HC + t:4 * (HC + K):4], T.gh[:, 4 * BOTH + t:4 * HC:4], T.hd[:, t:4 * K:4],
                           A.subtract, a_hd[t])

        def layer(h):
            a, b = half(h)
            k = quant(T.qz[:, a:b], T.sz[:, a:b], T.zz[:, 4 * a:4 * b], *[k_z[h, t] for t in range(4)])
            for t in range(4):
                p_r[h, t] = mm(4 * h + t, HC, T.qw[:, 128 * t:128 * t + 128], T.sw[:, 128 * t:128 * t + 128],
                               T.qz[:, a:b], T.sz[:, a:b], k, ("ldw", 32))

        def times32(h):
            if h == 0:
                for t in range(4):
                    a_z[h, t] = act(T.z32[:, t:4 * HC:4], T.zz[:, t:4 * HC:4], 32.0, k_z[h, t])
            else:
                k = act(T.z32[:, 4 * HC:4 * (HC + K)], T.zz[:, 4 * HC:4 * (HC + K)], 32.0, k_z[h, 1])
                a_z.update({(h, t): k for t in range(4)})

        def add(h, t):
            a, b = half(h)
            k_add.append(tt(plane(T.x32, t, a, b), T.pp[:, (4 * h + t) * BANK:(4 * h + t) * BANK + HC],
                            T.z32[:, 4 * a + t:4 * b:4], A.add, p_r[h, t], a_z[h, t]))

        for t in range(4):
            z_came(t)
        times32(0)
        for t in a_dg:
            a_hd[t] = ts(T.hd[:, t:4 * K:4], T.dg[:, t:4 * K:4], 0.5, A.mult)
        layer(0)
        for t in (2, 3, 0, 1):
            z_home(t)
        ts(T.z32[:, 4 * (HC + K):4 * C], T.zz[:, 4 * (HC + K):4 * C], 32.0, A.mult, k_both)
        times32(1)
        layer(1)
        for i in range(8):
            add(i // 4, i % 4)
        a_x = [act(T.xt[:, 4 * half(i // 4)[0] + i % 4:4 * half(i // 4)[1]:4], plane(T.x32, i % 4, *half(i // 4)),
                   1.0 / 32, k_add[i]) for i in range(NACT)]
        for t in range(NACT - 4, 4):
            k = ts(T.xt[:, 4 * HC + t:4 * C:4], plane(T.x32, t, HC, C), 1.0 / 32, A.mult, k_add[4 + t])
        k_x = [[a_x[3]], [a_x[-1], k]]
        if r == R - 1:
            a_od = act(T.odr[:], T.cols[:].indirect(go[:]), 1.0, g_cols)
            wait("act", a_od)
            g.scalar.dma_start(T.od[:], T.odr[0:128:16, :]).then_inc(S.outa, 16)

    g.sync.wait_ge(S.outs, 64)
    g.scalar.wait_ge(S.outa, 80)
    g.wait_ge(S.sent, sent[0])
    for q in ("dve", "act", "pe", "gp"):
        wait("gp", (q, count[q]))
